import numpy as np
import ml_dtypes


def mxq(x, axis, fmt="e4m3"):
    dtype, down = {"e4m3": (ml_dtypes.float8_e4m3fn, 7), "e5m2": (ml_dtypes.float8_e5m2, 14)}[fmt]
    v = np.moveaxis(np.asarray(x, np.float32).astype(ml_dtypes.bfloat16).astype(np.float64), axis, -1)
    blocks = v.reshape(v.shape[:-1] + (-1, 32))
    amax = np.abs(blocks).max(-1, keepdims=True)
    byte = np.maximum(np.where(amax > 0, np.frexp(amax)[1] - 1 + 127, 0) - down, 1)
    scale = np.exp2(byte - 127.0)
    codes = (blocks / scale).astype(np.float32).astype(dtype).astype(np.float64)
    return np.moveaxis((codes * scale).reshape(v.shape), -1, axis)


WIDE = False


def mx_kscale(k):
    if not WIDE:
        return np.ones(k)
    levels = np.array([10, -10, 5, -5, 0])
    if k % 512:
        return np.exp2(np.random.permutation(np.resize(levels, k // 32))).repeat(32)
    a = np.empty((k // 512, 16))
    for p in range(k // 512):
        a[p, :8] = np.random.permutation(np.resize(levels, 8))
        for g in range(8):
            far = levels[np.abs(levels - a[p, g]) >= 10]
            a[p, g + 8] = far[np.random.randint(len(far))]
    return np.exp2(a.ravel()).repeat(32)


def f64(x):
    return np.asarray(x).astype(np.float64)


def striped(idx):
    return np.tile(idx.reshape(-1, 16).T, (8, 1)).astype(np.uint16)


def unstriped(offs):
    return offs[:16].T.reshape(-1).astype(np.int64)


def silu(v):
    return v / (1.0 + np.exp(-np.maximum(v, -700.0)))


K, T, E, C, N = 2048, 768, 9, 256, 128
TOP = 3


def by_expert(wq, xq):
    return np.concatenate([wq[e].T @ xq[:, e * C:(e + 1) * C] for e in range(E)], axis=1)


def setup_inputs():
    n = np.random.standard_normal
    s = mx_kscale(K)[:, None]
    deal = np.repeat(np.arange(E), C).reshape(TOP, T)[:, np.random.permutation(T)]
    deal = np.take_along_axis(deal, np.argsort(np.random.rand(TOP, T), axis=0), axis=0)
    for _ in range(8):
        s_, t_ = np.random.permutation(T).reshape(2, -1); r = np.random.randint(TOP, size=T // 2); x, y = deal[r, s_].copy(), deal[r, t_].copy()
        ok = ~((deal[:, s_] == y).any(0) | (deal[:, t_] == x).any(0)); deal[r[ok], s_[ok]] = y[ok]; deal[r[ok], t_[ok]] = x[ok]
    order = np.lexsort((np.random.rand(TOP * T), deal.reshape(-1)))
    slot_token = order % T; pos = np.empty(TOP * T, np.int64); pos[order] = np.arange(TOP * T); pos = pos.reshape(TOP, T)
    g = np.random.uniform(0.5, 1.5, (TOP, T)); g = g / g.sum(0)
    return {
        "xT": (n((K, T)) * s).astype(np.float32),
        "w": (n((E + 1, K, N)) / np.sqrt(K) / s[None]).astype(np.float32),
        "b": (0.3 * n((N, E + 1))).astype(np.float32),
        "gate": np.stack([np.tile(r, (N, 1)) for r in g]).astype(np.float32),
        "offs": striped(slot_token),
        "pos1": striped(pos[0]),
        "pos2": striped(pos[1]),
        "pos3": striped(pos[2]),
    }


def reference(xT, w, b, gate, offs, pos1, pos2, pos3):
    idx = unstriped(offs)
    wq = mxq(f64(w), 1, "e4m3")
    xs = mxq(f64(xT), 0, "e4m3")
    ys = silu((wq[E].T @ xs) + f64(b)[:, E:])
    xq = mxq(f64(xT)[:, idx], 0, "e4m3")
    y = by_expert(wq, xq)
    y = silu(y + np.repeat(f64(b)[:, :E], C, axis=1))
    return ys + sum(f64(gate[r]) * y[:, unstriped(p)] for r, p in enumerate((pos1, pos2, pos3)))

@@ -1,0 +1,204 @@
+from contextlib import ExitStack
+
+import concourse.mybir as mybir
+
+K, T, E, C, N = 2048, 768, 9, 256, 128
+SLOTS = E * C
+FLOPS = 2 * K * N * (SLOTS + T)
+
+F32 = mybir.dt.float32
+BF16 = mybir.dt.bfloat16
+U32 = mybir.dt.uint32
+U16 = mybir.dt.uint16
+U8 = mybir.dt.uint8
+FP8X4 = mybir.dt.float8_e4m3fn_x4
+MULT = mybir.AluOpType.mult
+ADD = mybir.AluOpType.add
+SILU = mybir.ActivationFunctionType.Silu
+
+P = 128
+PACK = 4
+K_PASS = P * PACK
+PASSES = K // K_PASS
+CHUNK = 768
+CHUNKS = SLOTS // CHUNK
+PER_CHUNK = CHUNK // C
+WINDOW = 1024
+HALF = T // 2
+
+
+def tile_moe_shr_lin_silu_kernel(tc, xT, w, b, gate, offs, pos1, pos2, pos3, out):
+    nc = tc.nc
+    with ExitStack() as ctx:
+        keep = ctx.enter_context(tc.tile_pool(name="keep", bufs=1))
+        ring = ctx.enter_context(tc.tile_pool(name="ring", bufs=2))
+        psum = ctx.enter_context(tc.psum_pool(name="psum", bufs=1))
+
+        offs_sb = keep.tile([P, SLOTS // 16], U16, name="offs_sb")
+        pos_sb = [keep.tile([P, T // 16], U16, name="pos_sb%d" % r) for r in range(3)]
+        b_sb = keep.tile([P, E + 1], F32, name="b_sb")
+        y = keep.tile([P, SLOTS], F32, name="y")
+        ys = keep.tile([P, T], F32, name="ys")
+        planes = [keep.tile([P, 4 * WINDOW], BF16, name="planes%d" % i, align_bytes=64) for i in range(2)]
+        codes = {}
+        scales = {}
+        for g in range(PASSES):
+            for c in range(CHUNKS + 1):
+                codes[g, c] = keep.tile([P, CHUNK], U32, name="codes%d_%d" % (g, c), align_bytes=64)
+                scales[g, c] = keep.tile([P, CHUNK], U8, name="scales%d_%d" % (g, c), align_bytes=64)
+        w_codes = [keep.tile([P, PASSES * N], U32, name="w_codes%d" % e, align_bytes=64) for e in range(E + 1)]
+        w_scales = [keep.tile([P, PASSES * N], U8, name="w_scales%d" % e, align_bytes=64) for e in range(E + 1)]
+
+        def plane_of(g, h):
+            return planes[g % 2][:, 2 * WINDOW * h : 2 * WINDOW * (h + 1)]
+
+        for g in range(2):
+            for h in range(2):
+                nc.gpsimd.memset(plane_of(g, h)[:, 2 * T :].bitcast(U32), 0)
+
+        x_raw = {}
+        w_raw = {}
+
+        def load_x(g, h):
+            x_raw[g, h] = ring.tile([P, 2, T], F32, name="x_raw", bufs=4)
+            rows = xT[g * K_PASS : (g + 1) * K_PASS, :].rearrange("(p j) t -> p j t", j=PACK)
+            nc.sync.dma_start(out=x_raw[g, h][:], in_=rows[:, 2 * h : 2 * h + 2, :])
+
+        def load_w(e):
+            w_raw[e] = ring.tile([P, PASSES, PACK * N], F32, name="w_raw", bufs=4)
+            nc.sync.dma_start(out=w_raw[e][:], in_=w[e].rearrange("(g p j) n -> p g (j n)", p=P, j=PACK))
+
+        def cast_x(g, h, on_vector=False):
+            dst = plane_of(g, h)[:, : 2 * T].rearrange("p (t j) -> p t j", j=2)
+            src = x_raw[g, h][:].rearrange("p j t -> p t j")
+            if on_vector:
+                nc.vector.tensor_copy(out=dst, in_=src)
+            else:
+                nc.scalar.copy(out=dst, in_=src)
+
+        def cast_w(e):
+            w_bf = ring.tile([P, PASSES * N * PACK], BF16, name="w_bf", align_bytes=64)
+            nc.scalar.copy(
+                out=w_bf[:].rearrange("p (g c i j) -> p g c j i", g=PASSES, i=4, j=PACK),
+                in_=w_raw[e][:].rearrange("p g (j c i) -> p g c j i", j=PACK, i=4),
+            )
+            nc.vector.quantize_mx(out=w_codes[e][:].bitcast(FP8X4), scales=w_scales[e][:], in_=w_bf[:])
+
+        gathered = {}
+
+        def gather(g, c):
+            gathered[g, c] = ring.tile([P, 2, CHUNK], U32, name="gathered")
+            cols = slice(c * CHUNK // 16, (c + 1) * CHUNK // 16)
+            for h in range(2):
+                nc.vector.tensor_copy(
+                    out=gathered[g, c][:, h, :], in_=plane_of(g, h).bitcast(U32).indirect(offs_sb[:, cols])
+                )
+
+        def quantize(g, c, woven):
+            for lo, hi in ((0, 512), (512, CHUNK)):
+                nc.vector.quantize_mx(
+                    out=codes[g, c][:, lo:hi].bitcast(FP8X4),
+                    scales=scales[g, c][:, lo:hi],
+                    in_=woven[:, PACK * lo : PACK * hi],
+                )
+
+        def weave(g, c):
+            woven = ring.tile([P, PACK * CHUNK], BF16, name="woven", bufs=3, align_bytes=64)
+            nc.scalar.copy(
+                out=woven[:].bitcast(U32).rearrange("p (s h) -> p s h", h=2),
+                in_=gathered[g, c][:].rearrange("p h s -> p s h"),
+            )
+            quantize(g, c, woven)
+
+        def weave_shared(g):
+            woven = ring.tile([P, PACK * CHUNK], BF16, name="woven", bufs=3, align_bytes=64)
+            words = woven[:].bitcast(U32).rearrange("p (s h) -> p s h", h=2)
+            nc.scalar.copy(out=words, in_=planes[g % 2][:].bitcast(U32).rearrange("p (h s) -> p s h", h=2)[:, :T, :])
+            quantize(g, CHUNKS, woven)
+
+        def product(e, c, lo, width, acc, dst):
+            for g in range(PASSES):
+                nc.tensor.matmul_mx(
+                    out=acc[:],
+                    lhsT=w_codes[e][:, g * N : (g + 1) * N].bitcast(FP8X4),
+                    lhsT_scale=w_scales[e][:, g * N : (g + 1) * N],
+                    rhs=codes[g, c][:, lo : lo + width].bitcast(FP8X4),
+                    rhs_scale=scales[g, c][:, lo : lo + width],
+                    start=(g == 0),
+                    stop=(g == PASSES - 1),
+                )
+            nc.scalar.activation(out=dst, in_=acc[:], func=SILU, bias=b_sb[:, e : e + 1])
+
+        def experts(c):
+            for i in range(PER_CHUNK):
+                e = c * PER_CHUNK + i
+                acc = psum.tile([P, C], F32, name="acc", bufs=6)
+                product(e, c, i * C, C, acc, y[:, e * C : (e + 1) * C])
+
+        def shared():
+            for lo, width in ((0, 512), (512, 256)):
+                acc_shared = psum.tile([P, width], F32, name="acc_shared", bufs=2)
+                product(E, CHUNKS, lo, width, acc_shared, ys[:, lo : lo + width])
+
+        load_x(0, 0)
+        load_x(0, 1)
+        nc.sync.dma_start(offs_sb[:], offs)
+        load_w(0)
+        load_x(1, 0)
+        load_x(1, 1)
+        load_w(1)
+        load_w(2)
+        load_w(3)
+        nc.sync.dma_start(b_sb[:], b)
+        for r, pos in enumerate((pos1, pos2, pos3)):
+            nc.sync.dma_start(pos_sb[r][:], pos)
+
+        cast_x(0, 0, on_vector=True)
+        cast_x(0, 1)
+        w_order = {0: [0, 1, 2], 1: [3, 4, 5], 2: [6, 7, 8], 3: [9]}
+        next_w = 4
+        for g in range(PASSES):
+            todo = w_order[g]
+            if g == 0:
+                gather(0, 0)
+            for c in range(CHUNKS):
+                last = g == PASSES - 1 and c == CHUNKS - 1
+                if c < len(todo):
+                    cast_w(todo[c])
+                    if next_w <= E:
+                        load_w(next_w)
+                        next_w = next_w + 1
+                if c + 1 < CHUNKS:
+                    gather(g, c + 1)
+                if g + 1 < PASSES and c >= 1:
+                    cast_x(g + 1, c - 1)
+                    if g + 2 < PASSES:
+                        load_x(g + 2, c - 1)
+                if c + 1 == CHUNKS and g + 1 < PASSES:
+                    gather(g + 1, 0)
+                if last:
+                    weave_shared(g)
+                weave(g, c)
+                if g == PASSES - 1:
+                    experts(c)
+            if g < PASSES - 1:
+                weave_shared(g)
+        shared()
+
+        gate_a = ring.tile([P, 2, T], F32, name="x_raw", bufs=4)
+        nc.sync.dma_start(out=gate_a[:], in_=gate[0:2].rearrange("r n t -> n r t"))
+        gate_b = ring.tile([P, 2, T], F32, name="x_raw", bufs=4)
+        nc.sync.dma_start(out=gate_b[:, 0, :], in_=gate[2])
+        gates = [gate_a[:, 0, :], gate_a[:, 1, :], gate_b[:, 0, :]]
+
+        for half in range(2):
+            cols = slice(half * HALF, (half + 1) * HALF)
+            list_cols = slice(half * HALF // 16, (half + 1) * HALF // 16)
+            terms = ring.tile([P, 3, HALF], F32, name="terms")
+            sums = ring.tile([P, 3, HALF], F32, name="sums")
+            for r in range(3):
+                nc.vector.tensor_tensor(terms[:, r, :], y[:].indirect(pos_sb[r][:, list_cols]), gates[r][:, cols], MULT)
+            nc.vector.tensor_tensor(sums[:, 0, :], terms[:, 0, :], ys[:, cols], ADD)
+            nc.vector.tensor_tensor(sums[:, 1, :], terms[:, 1, :], terms[:, 2, :], ADD)
+            nc.vector.tensor_tensor(sums[:, 2, :], sums[:, 0, :], sums[:, 1, :], ADD)
+            nc.sync.dma_start(out=out[:, cols], in_=sums[:, 2, :])

@@ -14,6 +14,7 @@ U8 = mybir.dt.uint8
 FP8X4 = mybir.dt.float8_e4m3fn_x4
 MULT = mybir.AluOpType.mult
 ADD = mybir.AluOpType.add
+COPY = mybir.ActivationFunctionType.Copy
 SILU = mybir.ActivationFunctionType.Silu
 
 P = 128
@@ -25,6 +26,14 @@ CHUNKS = SLOTS // CHUNK
 PER_CHUNK = CHUNK // C
 WINDOW = 1024
 HALF = T // 2
+
+
+UNITS = PASSES * CHUNKS
+LAST = PASSES - 1
+W_COLS = PASSES * N
+ROW_W = 4
+ROW_SHARED = 8
+ROW_W_SHARED = 12
 
 
 def tile_moe_shr_lin_silu_kernel(tc, xT, w, b, gate, offs, pos1, pos2, pos3, out):
@@ -40,14 +49,19 @@ def tile_moe_shr_lin_silu_kernel(tc, xT, w, b, gate, offs, pos1, pos2, pos3, out
         y = keep.tile([P, SLOTS], F32, name="y")
         ys = keep.tile([P, T], F32, name="ys")
         planes = [keep.tile([P, 4 * WINDOW], BF16, name="planes%d" % i, align_bytes=64) for i in range(2)]
-        codes = {}
-        scales = {}
-        for g in range(PASSES):
-            for c in range(CHUNKS + 1):
-                codes[g, c] = keep.tile([P, CHUNK], U32, name="codes%d_%d" % (g, c), align_bytes=64)
-                scales[g, c] = keep.tile([P, CHUNK], U8, name="scales%d_%d" % (g, c), align_bytes=64)
-        w_codes = [keep.tile([P, PASSES * N], U32, name="w_codes%d" % e, align_bytes=64) for e in range(E + 1)]
-        w_scales = [keep.tile([P, PASSES * N], U8, name="w_scales%d" % e, align_bytes=64) for e in range(E + 1)]
+        singles = keep.tile([P, 2 * WINDOW], BF16, name="singles", align_bytes=64)
+        stage = [keep.tile([P, 2 * CHUNK], U32, name="stage%d" % i, align_bytes=64) for i in range(3)]
+        late = [keep.tile([P, 3 * CHUNK], U32, name="late%d" % c, align_bytes=64) for c in range(CHUNKS)]
+        shared_stage = keep.tile([P, 2 * T], U32, name="shared_stage", align_bytes=64)
+        w_bf = [keep.tile([P, PACK * T], BF16, name="w_bf%d" % i, align_bytes=64) for i in range(2)]
+        codes = [keep.tile([P, CHUNK], U32, name="codes%d" % u, align_bytes=64) for u in range(UNITS)]
+        scale_rows = [keep.tile([P, C + CHUNK], U8, name="scale_rows%d" % u, align_bytes=64) for u in range(UNITS)]
+        scales = [rows[:, C:] for rows in scale_rows]
+        shared_codes = [keep.tile([P, T], U32, name="shared_codes%d" % g, align_bytes=64) for g in range(PASSES)]
+        w_codes = [keep.tile([P, W_COLS], U32, name="w_codes%d" % e, align_bytes=64) for e in range(E + 1)]
+        shared_scales = [scale_rows[u][ROW_SHARED:, C:] for u in (0, 3, UNITS - 1)]
+        shared_scales.append(scale_rows[UNITS - 1][ROW_W_SHARED:, C:])
+        w_scales = {}
 
         def plane_of(g, h):
             return planes[g % 2][:, 2 * WINDOW * h : 2 * WINDOW * (h + 1)]
@@ -55,6 +69,8 @@ def tile_moe_shr_lin_silu_kernel(tc, xT, w, b, gate, offs, pos1, pos2, pos3, out
         for g in range(2):
             for h in range(2):
                 nc.gpsimd.memset(plane_of(g, h)[:, 2 * T :].bitcast(U32), 0)
+        for j in range(2):
+            nc.gpsimd.memset(singles[:, j * WINDOW + T : (j + 1) * WINDOW].bitcast(U32), 0)
 
         x_raw = {}
         w_raw = {}
@@ -70,119 +86,189 @@ def tile_moe_shr_lin_silu_kernel(tc, xT, w, b, gate, offs, pos1, pos2, pos3, out
 
         def cast_x(g, h, on_vector=False):
             dst = plane_of(g, h)[:, : 2 * T].rearrange("p (t j) -> p t j", j=2)
-            src = x_raw[g, h][:].rearrange("p j t -> p t j")
+            if (g, h) == (LAST, 1):
+                src = singles[:].rearrange("p (j s) -> p s j", j=2)[:, :T, :]
+            else:
+                src = x_raw[g, h][:].rearrange("p j t -> p t j")
             if on_vector:
                 nc.vector.tensor_copy(out=dst, in_=src)
             else:
                 nc.scalar.copy(out=dst, in_=src)
 
-        def cast_w(e):
-            w_bf = ring.tile([P, PASSES * N * PACK], BF16, name="w_bf", align_bytes=64)
+        def cast_singles():
+            nc.scalar.copy(out=singles[:].rearrange("p (j s) -> p j s", j=2)[:, :, :T], in_=x_raw[LAST, 1][:])
+
+        def cast_w_scalar(e, dst):
             nc.scalar.copy(
-                out=w_bf[:].rearrange("p (g c i j) -> p g c j i", g=PASSES, i=4, j=PACK),
+                out=dst.rearrange("p (g c i j) -> p g c j i", g=PASSES, i=4, j=PACK),
                 in_=w_raw[e][:].rearrange("p g (j c i) -> p g c j i", j=PACK, i=4),
             )
-            nc.vector.quantize_mx(out=w_codes[e][:].bitcast(FP8X4), scales=w_scales[e][:], in_=w_bf[:])
 
-        gathered = {}
-
-        def gather(g, c):
-            gathered[g, c] = ring.tile([P, 2, CHUNK], U32, name="gathered")
-            cols = slice(c * CHUNK // 16, (c + 1) * CHUNK // 16)
-            for h in range(2):
-                nc.vector.tensor_copy(
-                    out=gathered[g, c][:, h, :], in_=plane_of(g, h).bitcast(U32).indirect(offs_sb[:, cols])
-                )
-
-        def quantize(g, c, woven):
-            for lo, hi in ((0, 512), (512, CHUNK)):
-                nc.vector.quantize_mx(
-                    out=codes[g, c][:, lo:hi].bitcast(FP8X4),
-                    scales=scales[g, c][:, lo:hi],
-                    in_=woven[:, PACK * lo : PACK * hi],
-                )
-
-        def weave(g, c):
-            woven = ring.tile([P, PACK * CHUNK], BF16, name="woven", bufs=3, align_bytes=64)
-            nc.scalar.copy(
-                out=woven[:].bitcast(U32).rearrange("p (s h) -> p s h", h=2),
-                in_=gathered[g, c][:].rearrange("p h s -> p s h"),
+        def cast_w_gpsimd(e, g0, g1, dst):
+            nc.gpsimd.tensor_scalar(
+                dst[:, : (g1 - g0) * N * PACK].rearrange("p (g n j) -> p g n j", n=N, j=PACK),
+                w_raw[e][:, g0:g1, :].rearrange("p g (j n) -> p g n j", j=PACK),
+                1.0,
+                0.0,
+                MULT,
+                ADD,
             )
-            quantize(g, c, woven)
 
-        def weave_shared(g):
-            woven = ring.tile([P, PACK * CHUNK], BF16, name="woven", bufs=3, align_bytes=64)
-            words = woven[:].bitcast(U32).rearrange("p (s h) -> p s h", h=2)
-            nc.scalar.copy(out=words, in_=planes[g % 2][:].bitcast(U32).rearrange("p (h s) -> p s h", h=2)[:, :T, :])
-            quantize(g, CHUNKS, woven)
+        def quantize_w(e, g0, g1, src, plane):
+            width = (g1 - g0) * N
+            nc.vector.quantize_mx(
+                out=w_codes[e][:, g0 * N : g1 * N].bitcast(FP8X4), scales=plane[:, :width], in_=src[:, : PACK * width]
+            )
+            for g in range(g0, g1):
+                w_scales[e, g] = plane[:, (g - g0) * N : (g - g0 + 1) * N]
 
-        def product(e, c, lo, width, acc, dst):
+        def gathered(u):
+            g, c = divmod(u, CHUNKS)
+            return late[c][:, CHUNK:] if g == LAST else stage[u % 3][:]
+
+        def woven(u):
+            if LAST * CHUNKS - 2 <= u < UNITS - 2:
+                return late[u + 2 - LAST * CHUNKS][:, : 2 * CHUNK]
+            return stage[(u + 2) % 3][:]
+
+        def list_cols(c):
+            return offs_sb[:, c * CHUNK // 16 : (c + 1) * CHUNK // 16]
+
+        def gather(u):
+            g, c = divmod(u, CHUNKS)
+            for h in range(1 if g == LAST else 2):
+                nc.vector.tensor_copy(
+                    out=gathered(u)[:, h * CHUNK : (h + 1) * CHUNK],
+                    in_=plane_of(g, h).bitcast(U32).indirect(list_cols(c)),
+                )
+
+        def gather_on_scalar(c, j):
+            pairs = late[c][:, 2 * CHUNK :].bitcast(BF16).rearrange("p (s j) -> p s j", j=2)
+            nc.scalar.activation(
+                out=pairs[:, :, j], in_=singles[:, j * WINDOW : (j + 1) * WINDOW].indirect(list_cols(c)), func=COPY
+            )
+
+        def quantize(dst, plane, src, lo, hi):
+            nc.vector.quantize_mx(
+                out=dst[:, lo:hi].bitcast(FP8X4), scales=plane[:, lo:hi], in_=src.bitcast(BF16)[:, PACK * lo : PACK * hi]
+            )
+
+        def weave(src, dst, lo, hi):
+            nc.scalar.copy(
+                out=dst.rearrange("p (s h) -> p s h", h=2)[:, lo:hi, :],
+                in_=src.rearrange("p (h s) -> p s h", h=2)[:, lo:hi, :],
+            )
+
+        def weave_shared(g, dst):
+            weave(planes[g % 2][:].bitcast(U32), dst, 0, T)
+
+        def quantize_shared(g, src):
+            quantize(shared_codes[g], shared_scales[g], src, 0, 512)
+            quantize(shared_codes[g], shared_scales[g], src, 512, T)
+
+        def product(e, operands, lo, width, acc, dst):
             for g in range(PASSES):
+                moving, plane = operands[g]
                 nc.tensor.matmul_mx(
                     out=acc[:],
                     lhsT=w_codes[e][:, g * N : (g + 1) * N].bitcast(FP8X4),
-                    lhsT_scale=w_scales[e][:, g * N : (g + 1) * N],
-                    rhs=codes[g, c][:, lo : lo + width].bitcast(FP8X4),
-                    rhs_scale=scales[g, c][:, lo : lo + width],
+                    lhsT_scale=w_scales[e, g],
+                    rhs=moving[:, lo : lo + width].bitcast(FP8X4),
+                    rhs_scale=plane[:, lo : lo + width],
                     start=(g == 0),
-                    stop=(g == PASSES - 1),
+                    stop=(g == LAST),
                 )
             nc.scalar.activation(out=dst, in_=acc[:], func=SILU, bias=b_sb[:, e : e + 1])
 
-        def experts(c):
-            for i in range(PER_CHUNK):
-                e = c * PER_CHUNK + i
-                acc = psum.tile([P, C], F32, name="acc", bufs=6)
-                product(e, c, i * C, C, acc, y[:, e * C : (e + 1) * C])
+        def expert(e):
+            c, i = divmod(e, PER_CHUNK)
+            acc = psum.tile([P, C], F32, name="acc", bufs=6)
+            operands = [(codes[g * CHUNKS + c], scales[g * CHUNKS + c]) for g in range(PASSES)]
+            product(e, operands, i * C, C, acc, y[:, e * C : (e + 1) * C])
 
         def shared():
+            operands = [(shared_codes[g], shared_scales[g]) for g in range(PASSES)]
             for lo, width in ((0, 512), (512, 256)):
                 acc_shared = psum.tile([P, width], F32, name="acc_shared", bufs=2)
-                product(E, CHUNKS, lo, width, acc_shared, ys[:, lo : lo + width])
+                product(E, operands, lo, width, acc_shared, ys[:, lo : lo + width])
 
         load_x(0, 0)
-        load_x(0, 1)
         nc.sync.dma_start(offs_sb[:], offs)
+        load_x(0, 1)
         load_w(0)
         load_x(1, 0)
-        load_x(1, 1)
         load_w(1)
-        load_w(2)
-        load_w(3)
+        load_x(1, 1)
         nc.sync.dma_start(b_sb[:], b)
         for r, pos in enumerate((pos1, pos2, pos3)):
             nc.sync.dma_start(pos_sb[r][:], pos)
 
         cast_x(0, 0, on_vector=True)
         cast_x(0, 1)
-        w_order = {0: [0, 1, 2], 1: [3, 4, 5], 2: [6, 7, 8], 3: [9]}
-        next_w = 4
-        for g in range(PASSES):
-            todo = w_order[g]
-            if g == 0:
-                gather(0, 0)
-            for c in range(CHUNKS):
-                last = g == PASSES - 1 and c == CHUNKS - 1
-                if c < len(todo):
-                    cast_w(todo[c])
-                    if next_w <= E:
-                        load_w(next_w)
-                        next_w = next_w + 1
-                if c + 1 < CHUNKS:
-                    gather(g, c + 1)
-                if g + 1 < PASSES and c >= 1:
-                    cast_x(g + 1, c - 1)
-                    if g + 2 < PASSES:
-                        load_x(g + 2, c - 1)
-                if c + 1 == CHUNKS and g + 1 < PASSES:
-                    gather(g + 1, 0)
-                if last:
-                    weave_shared(g)
-                weave(g, c)
-                if g == PASSES - 1:
-                    experts(c)
-            if g < PASSES - 1:
-                weave_shared(g)
+        load_x(LAST, 1)
+        load_w(2)
+        load_x(2, 0)
+        load_w(3)
+        gather(0)
+        gather(1)
+        w_cast = [buf[:, PACK * (T - W_COLS) :] for buf in w_bf]
+        cast_w_gpsimd(0, 0, PASSES, w_cast[0])
+        weave_shared(0, w_bf[1][:].bitcast(U32))
+        w_shared_bf = late[2][:, : 2 * W_COLS].bitcast(BF16)
+
+        fillers = {
+            0: [lambda: cast_x(1, 0), lambda: load_x(2, 1), cast_singles, lambda: load_x(LAST, 0)],
+            1: [lambda: cast_x(1, 1), lambda: gather_on_scalar(0, 0)],
+            2: [lambda: gather_on_scalar(0, 1), lambda: weave_shared(1, shared_stage[:])],
+            3: [lambda: cast_x(2, 0), lambda: gather_on_scalar(1, 0)],
+            4: [lambda: cast_x(2, 1), lambda: gather_on_scalar(1, 1)],
+            5: [lambda: cast_w_scalar(E, w_shared_bf)],
+            6: [lambda: cast_x(LAST, 0), lambda: gather_on_scalar(2, 0)],
+            7: [lambda: cast_x(LAST, 1), lambda: gather_on_scalar(2, 1)],
+            8: [lambda: weave_shared(2, shared_stage[:])],
+            9: [lambda: weave_shared(LAST, stage[2][:])],
+        }
+        order_w = [0, 1, 2, 3, 4, 5, E, 6, 7, 8]
+        loaded = 4
+        for u in range(UNITS - 1):
+            g, c = divmod(u, CHUNKS)
+            weave(gathered(u), woven(u), 0, CHUNK)
+            if u == 3:
+                quantize_shared(1, shared_stage[:])
+            quantize(codes[u], scales[u], woven(u), 0, C)
+            quantize(codes[u], scales[u], woven(u), C, 2 * C)
+            if u == 6:
+                quantize_w(E, 0, PASSES, w_shared_bf, scale_rows[u][ROW_W_SHARED:, :])
+            if 1 <= u < E:
+                quantize_w(u - 1, 0, PASSES, w_cast[(u - 1) % 2], scale_rows[u][ROW_W:, :])
+            elif u >= E:
+                half = u - E
+                quantize_w(E - 1, 2 * half, 2 * half + 2, w_cast[half], scale_rows[u][ROW_W:, C:])
+            quantize(codes[u], scales[u], woven(u), 2 * C, CHUNK)
+            if u == 0:
+                quantize_shared(0, w_bf[1][:].bitcast(U32))
+            if loaded <= E:
+                load_w(order_w[loaded])
+                loaded = loaded + 1
+            for job in fillers.get(u, ()):
+                job()
+            if u + 2 < UNITS:
+                gather(u + 2)
+            if u < E - 2:
+                cast_w_gpsimd(u + 1, 0, PASSES, w_cast[(u + 1) % 2])
+            elif u < E:
+                half = u - (E - 2)
+                cast_w_gpsimd(E - 1, 2 * half, 2 * half + 2, w_cast[half])
+        for e in range(PER_CHUNK):
+            expert(e)
+        u = UNITS - 1
+        for i in range(PER_CHUNK):
+            weave(gathered(u), woven(u), i * C, (i + 1) * C)
+            quantize(codes[u], scales[u], woven(u), i * C, (i + 1) * C)
+        for e in range(PER_CHUNK, E):
+            expert(e)
+        quantize_shared(2, shared_stage[:])
+        quantize_shared(LAST, stage[2][:])
         shared()
 
         gate_a = ring.tile([P, 2, T], F32, name="x_raw", bufs=4)
@@ -193,12 +279,11 @@ def tile_moe_shr_lin_silu_kernel(tc, xT, w, b, gate, offs, pos1, pos2, pos3, out
 
         for half in range(2):
             cols = slice(half * HALF, (half + 1) * HALF)
-            list_cols = slice(half * HALF // 16, (half + 1) * HALF // 16)
-            terms = ring.tile([P, 3, HALF], F32, name="terms")
-            sums = ring.tile([P, 3, HALF], F32, name="sums")
+            pos_cols = slice(half * HALF // 16, (half + 1) * HALF // 16)
+            parts = late[half][:].bitcast(F32).rearrange("p (r t) -> p r t", t=HALF)
             for r in range(3):
-                nc.vector.tensor_tensor(terms[:, r, :], y[:].indirect(pos_sb[r][:, list_cols]), gates[r][:, cols], MULT)
-            nc.vector.tensor_tensor(sums[:, 0, :], terms[:, 0, :], ys[:, cols], ADD)
-            nc.vector.tensor_tensor(sums[:, 1, :], terms[:, 1, :], terms[:, 2, :], ADD)
-            nc.vector.tensor_tensor(sums[:, 2, :], sums[:, 0, :], sums[:, 1, :], ADD)
-            nc.sync.dma_start(out=out[:, cols], in_=sums[:, 2, :])
+                nc.vector.tensor_tensor(parts[:, r, :], y[:].indirect(pos_sb[r][:, pos_cols]), gates[r][:, cols], MULT)
+            nc.vector.tensor_tensor(parts[:, 3, :], parts[:, 0, :], parts[:, 1, :], ADD)
+            nc.vector.tensor_tensor(parts[:, 4, :], parts[:, 3, :], parts[:, 2, :], ADD)
+            nc.vector.tensor_tensor(parts[:, 5, :], parts[:, 4, :], ys[:, cols], ADD)
+            nc.sync.dma_start(out=out[:, cols], in_=parts[:, 5, :])

@@ -14,7 +14,6 @@ U8 = mybir.dt.uint8
 FP8X4 = mybir.dt.float8_e4m3fn_x4
 MULT = mybir.AluOpType.mult
 ADD = mybir.AluOpType.add
-COPY = mybir.ActivationFunctionType.Copy
 SILU = mybir.ActivationFunctionType.Silu
 
 P = 128
@@ -34,13 +33,14 @@ W_COLS = PASSES * N
 ROW_W = 4
 ROW_SHARED = 8
 ROW_W_SHARED = 12
+GPSIMD_COLS = 80
 
 
 def tile_moe_shr_lin_silu_kernel(tc, xT, w, b, gate, offs, pos1, pos2, pos3, out):
     nc = tc.nc
     with ExitStack() as ctx:
         keep = ctx.enter_context(tc.tile_pool(name="keep", bufs=1))
-        ring = ctx.enter_context(tc.tile_pool(name="ring", bufs=2))
+        ring = ctx.enter_context(tc.tile_pool(name="ring", bufs=4))
         psum = ctx.enter_context(tc.psum_pool(name="psum", bufs=1))
 
         offs_sb = keep.tile([P, SLOTS // 16], U16, name="offs_sb")
@@ -49,19 +49,21 @@ def tile_moe_shr_lin_silu_kernel(tc, xT, w, b, gate, offs, pos1, pos2, pos3, out
         y = keep.tile([P, SLOTS], F32, name="y")
         ys = keep.tile([P, T], F32, name="ys")
         planes = [keep.tile([P, 4 * WINDOW], BF16, name="planes%d" % i, align_bytes=64) for i in range(2)]
-        singles = keep.tile([P, 2 * WINDOW], BF16, name="singles", align_bytes=64)
         stage = [keep.tile([P, 2 * CHUNK], U32, name="stage%d" % i, align_bytes=64) for i in range(3)]
-        late = [keep.tile([P, 3 * CHUNK], U32, name="late%d" % c, align_bytes=64) for c in range(CHUNKS)]
-        shared_stage = keep.tile([P, 2 * T], U32, name="shared_stage", align_bytes=64)
         w_bf = [keep.tile([P, PACK * T], BF16, name="w_bf%d" % i, align_bytes=64) for i in range(2)]
+        shared_stage = [keep.tile([P, 2 * T], U32, name="shared_stage%d" % i, align_bytes=64) for i in range(2)]
+        shared_woven = [w_bf[1][:].bitcast(U32), shared_stage[1][:], shared_stage[0][:], shared_stage[1][:]]
+        w_cast = [buf[:, PACK * (T - W_COLS) :] for buf in w_bf]
         codes = [keep.tile([P, CHUNK], U32, name="codes%d" % u, align_bytes=64) for u in range(UNITS)]
         scale_rows = [keep.tile([P, C + CHUNK], U8, name="scale_rows%d" % u, align_bytes=64) for u in range(UNITS)]
         scales = [rows[:, C:] for rows in scale_rows]
         shared_codes = [keep.tile([P, T], U32, name="shared_codes%d" % g, align_bytes=64) for g in range(PASSES)]
         w_codes = [keep.tile([P, W_COLS], U32, name="w_codes%d" % e, align_bytes=64) for e in range(E + 1)]
-        shared_scales = [scale_rows[u][ROW_SHARED:, C:] for u in (0, 3, UNITS - 1)]
-        shared_scales.append(scale_rows[UNITS - 1][ROW_W_SHARED:, C:])
-        w_scales = {}
+        shared_scales = [scale_rows[u][ROW_SHARED:, :T] for u in (0, CHUNKS, UNITS - 1)]
+        shared_scales.append(scale_rows[UNITS - 1][ROW_W_SHARED:, :T])
+        w_order = [E] + list(range(E))
+        w_scales = {e: scale_rows[i + 1][(ROW_W if e < E else ROW_W_SHARED) :, :W_COLS] for i, e in enumerate(w_order)}
+        parts = [keep.tile([P, 6, HALF], F32, name="parts%d" % i) for i in range(2)]
 
         def plane_of(g, h):
             return planes[g % 2][:, 2 * WINDOW * h : 2 * WINDOW * (h + 1)]
@@ -69,84 +71,55 @@ def tile_moe_shr_lin_silu_kernel(tc, xT, w, b, gate, offs, pos1, pos2, pos3, out
         for g in range(2):
             for h in range(2):
                 nc.gpsimd.memset(plane_of(g, h)[:, 2 * T :].bitcast(U32), 0)
-        for j in range(2):
-            nc.gpsimd.memset(singles[:, j * WINDOW + T : (j + 1) * WINDOW].bitcast(U32), 0)
 
         x_raw = {}
         w_raw = {}
 
         def load_x(g, h):
-            x_raw[g, h] = ring.tile([P, 2, T], F32, name="x_raw", bufs=4)
+            x_raw[g, h] = ring.tile([P, 2, T], F32, name="x_raw")
             rows = xT[g * K_PASS : (g + 1) * K_PASS, :].rearrange("(p j) t -> p j t", j=PACK)
             nc.sync.dma_start(out=x_raw[g, h][:], in_=rows[:, 2 * h : 2 * h + 2, :])
 
-        def load_w(e):
-            w_raw[e] = ring.tile([P, PASSES, PACK * N], F32, name="w_raw", bufs=4)
-            nc.sync.dma_start(out=w_raw[e][:], in_=w[e].rearrange("(g p j) n -> p g (j n)", p=P, j=PACK))
+        def load_w(i):
+            w_raw[i] = ring.tile([P, PASSES, PACK * N], F32, name="w_raw")
+            nc.sync.dma_start(out=w_raw[i][:], in_=w[w_order[i]].rearrange("(g p j) n -> p g (j n)", p=P, j=PACK))
 
-        def cast_x(g, h, on_vector=False):
-            dst = plane_of(g, h)[:, : 2 * T].rearrange("p (t j) -> p t j", j=2)
-            if (g, h) == (LAST, 1):
-                src = singles[:].rearrange("p (j s) -> p s j", j=2)[:, :T, :]
-            else:
-                src = x_raw[g, h][:].rearrange("p j t -> p t j")
-            if on_vector:
-                nc.vector.tensor_copy(out=dst, in_=src)
-            else:
-                nc.scalar.copy(out=dst, in_=src)
-
-        def cast_singles():
-            nc.scalar.copy(out=singles[:].rearrange("p (j s) -> p j s", j=2)[:, :, :T], in_=x_raw[LAST, 1][:])
-
-        def cast_w_scalar(e, dst):
-            nc.scalar.copy(
-                out=dst.rearrange("p (g c i j) -> p g c j i", g=PASSES, i=4, j=PACK),
-                in_=w_raw[e][:].rearrange("p g (j c i) -> p g c j i", j=PACK, i=4),
+        def cast_x(g, h, copy):
+            copy(
+                out=plane_of(g, h)[:, : 2 * T].rearrange("p (t j) -> p t j", j=2),
+                in_=x_raw[g, h][:].rearrange("p j t -> p t j"),
             )
 
-        def cast_w_gpsimd(e, g0, g1, dst):
+        def cast_w_scalar(i):
+            first = GPSIMD_COLS // 4
+            nc.scalar.copy(
+                out=w_cast[i % 2].rearrange("p (g c i j) -> p g c j i", g=PASSES, i=4, j=PACK)[:, :, first:],
+                in_=w_raw[i][:].rearrange("p g (j c i) -> p g c j i", j=PACK, i=4)[:, :, first:],
+            )
+
+        def cast_w_gpsimd(i):
             nc.gpsimd.tensor_scalar(
-                dst[:, : (g1 - g0) * N * PACK].rearrange("p (g n j) -> p g n j", n=N, j=PACK),
-                w_raw[e][:, g0:g1, :].rearrange("p g (j n) -> p g n j", j=PACK),
+                w_cast[i % 2].rearrange("p (g n j) -> p g n j", n=N, j=PACK)[:, :, :GPSIMD_COLS],
+                w_raw[i][:].rearrange("p g (j n) -> p g n j", j=PACK)[:, :, :GPSIMD_COLS],
                 1.0,
                 0.0,
                 MULT,
                 ADD,
             )
 
-        def quantize_w(e, g0, g1, src, plane):
-            width = (g1 - g0) * N
-            nc.vector.quantize_mx(
-                out=w_codes[e][:, g0 * N : g1 * N].bitcast(FP8X4), scales=plane[:, :width], in_=src[:, : PACK * width]
-            )
-            for g in range(g0, g1):
-                w_scales[e, g] = plane[:, (g - g0) * N : (g - g0 + 1) * N]
-
         def gathered(u):
-            g, c = divmod(u, CHUNKS)
-            return late[c][:, CHUNK:] if g == LAST else stage[u % 3][:]
+            return stage[u % 3][:]
 
         def woven(u):
-            if LAST * CHUNKS - 2 <= u < UNITS - 2:
-                return late[u + 2 - LAST * CHUNKS][:, : 2 * CHUNK]
             return stage[(u + 2) % 3][:]
-
-        def list_cols(c):
-            return offs_sb[:, c * CHUNK // 16 : (c + 1) * CHUNK // 16]
 
         def gather(u):
             g, c = divmod(u, CHUNKS)
-            for h in range(1 if g == LAST else 2):
+            offsets = offs_sb[:, c * CHUNK // 16 : (c + 1) * CHUNK // 16]
+            for h in range(2):
                 nc.vector.tensor_copy(
-                    out=gathered(u)[:, h * CHUNK : (h + 1) * CHUNK],
-                    in_=plane_of(g, h).bitcast(U32).indirect(list_cols(c)),
+                    out=gathered(u)[:, h * CHUNK : (h + 1) * CHUNK], in_=plane_of(g, h).bitcast(U32).indirect(offsets)
                 )
-
-        def gather_on_scalar(c, j):
-            pairs = late[c][:, 2 * CHUNK :].bitcast(BF16).rearrange("p (s j) -> p s j", j=2)
-            nc.scalar.activation(
-                out=pairs[:, :, j], in_=singles[:, j * WINDOW : (j + 1) * WINDOW].indirect(list_cols(c)), func=COPY
-            )
 
         def quantize(dst, plane, src, lo, hi):
             nc.vector.quantize_mx(
@@ -159,12 +132,12 @@ def tile_moe_shr_lin_silu_kernel(tc, xT, w, b, gate, offs, pos1, pos2, pos3, out
                 in_=src.rearrange("p (h s) -> p s h", h=2)[:, lo:hi, :],
             )
 
-        def weave_shared(g, dst):
-            weave(planes[g % 2][:].bitcast(U32), dst, 0, T)
+        def weave_shared(g):
+            weave(planes[g % 2][:].bitcast(U32), shared_woven[g], 0, T)
 
-        def quantize_shared(g, src):
-            quantize(shared_codes[g], shared_scales[g], src, 0, 512)
-            quantize(shared_codes[g], shared_scales[g], src, 512, T)
+        def quantize_shared(g):
+            quantize(shared_codes[g], shared_scales[g], shared_woven[g], 0, 512)
+            quantize(shared_codes[g], shared_scales[g], shared_woven[g], 512, T)
 
         def product(e, operands, lo, width, acc, dst):
             for g in range(PASSES):
@@ -172,7 +145,7 @@ def tile_moe_shr_lin_silu_kernel(tc, xT, w, b, gate, offs, pos1, pos2, pos3, out
                 nc.tensor.matmul_mx(
                     out=acc[:],
                     lhsT=w_codes[e][:, g * N : (g + 1) * N].bitcast(FP8X4),
-                    lhsT_scale=w_scales[e, g],
+                    lhsT_scale=w_scales[e][:, g * N : (g + 1) * N],
                     rhs=moving[:, lo : lo + width].bitcast(FP8X4),
                     rhs_scale=plane[:, lo : lo + width],
                     start=(g == 0),
@@ -202,88 +175,85 @@ def tile_moe_shr_lin_silu_kernel(tc, xT, w, b, gate, offs, pos1, pos2, pos3, out
         nc.sync.dma_start(b_sb[:], b)
         for r, pos in enumerate((pos1, pos2, pos3)):
             nc.sync.dma_start(pos_sb[r][:], pos)
-
-        cast_x(0, 0, on_vector=True)
-        cast_x(0, 1)
-        load_x(LAST, 1)
         load_w(2)
-        load_x(2, 0)
         load_w(3)
+
+        cast_x(0, 0, nc.vector.tensor_copy)
+        cast_x(0, 1, nc.scalar.copy)
+        load_x(2, 0)
+        load_x(2, 1)
         gather(0)
         gather(1)
-        w_cast = [buf[:, PACK * (T - W_COLS) :] for buf in w_bf]
-        cast_w_gpsimd(0, 0, PASSES, w_cast[0])
-        weave_shared(0, w_bf[1][:].bitcast(U32))
-        w_shared_bf = late[2][:, : 2 * W_COLS].bitcast(BF16)
+        cast_w_gpsimd(0)
+        weave_shared(0)
 
-        fillers = {
-            0: [lambda: cast_x(1, 0), lambda: load_x(2, 1), cast_singles, lambda: load_x(LAST, 0)],
-            1: [lambda: cast_x(1, 1), lambda: gather_on_scalar(0, 0)],
-            2: [lambda: gather_on_scalar(0, 1), lambda: weave_shared(1, shared_stage[:])],
-            3: [lambda: cast_x(2, 0), lambda: gather_on_scalar(1, 0)],
-            4: [lambda: cast_x(2, 1), lambda: gather_on_scalar(1, 1)],
-            5: [lambda: cast_w_scalar(E, w_shared_bf)],
-            6: [lambda: cast_x(LAST, 0), lambda: gather_on_scalar(2, 0)],
-            7: [lambda: cast_x(LAST, 1), lambda: gather_on_scalar(2, 1)],
-            8: [lambda: weave_shared(2, shared_stage[:])],
-            9: [lambda: weave_shared(LAST, stage[2][:])],
-        }
-        order_w = [0, 1, 2, 3, 4, 5, E, 6, 7, 8]
-        loaded = 4
         for u in range(UNITS - 1):
             g, c = divmod(u, CHUNKS)
             weave(gathered(u), woven(u), 0, CHUNK)
-            if u == 3:
-                quantize_shared(1, shared_stage[:])
+            if u == CHUNKS:
+                quantize_shared(1)
             quantize(codes[u], scales[u], woven(u), 0, C)
             quantize(codes[u], scales[u], woven(u), C, 2 * C)
-            if u == 6:
-                quantize_w(E, 0, PASSES, w_shared_bf, scale_rows[u][ROW_W_SHARED:, :])
-            if 1 <= u < E:
-                quantize_w(u - 1, 0, PASSES, w_cast[(u - 1) % 2], scale_rows[u][ROW_W:, :])
-            elif u >= E:
-                half = u - E
-                quantize_w(E - 1, 2 * half, 2 * half + 2, w_cast[half], scale_rows[u][ROW_W:, C:])
+            if u >= 1:
+                e = w_order[u - 1]
+                nc.vector.quantize_mx(out=w_codes[e][:].bitcast(FP8X4), scales=w_scales[e], in_=w_cast[(u - 1) % 2])
             quantize(codes[u], scales[u], woven(u), 2 * C, CHUNK)
             if u == 0:
-                quantize_shared(0, w_bf[1][:].bitcast(U32))
-            if loaded <= E:
-                load_w(order_w[loaded])
-                loaded = loaded + 1
-            for job in fillers.get(u, ()):
-                job()
+                quantize_shared(0)
+            if g < LAST:
+                if c < 2:
+                    cast_x(g + 1, c, nc.scalar.copy)
+                    if g + 3 < PASSES:
+                        load_x(g + 3, c)
+                else:
+                    weave_shared(g + 1)
+            if u <= E:
+                cast_w_scalar(u)
+                if u + 4 <= E:
+                    load_w(u + 4)
             if u + 2 < UNITS:
                 gather(u + 2)
-            if u < E - 2:
-                cast_w_gpsimd(u + 1, 0, PASSES, w_cast[(u + 1) % 2])
-            elif u < E:
-                half = u - (E - 2)
-                cast_w_gpsimd(E - 1, 2 * half, 2 * half + 2, w_cast[half])
+            if u + 1 <= E:
+                cast_w_gpsimd(u + 1)
         for e in range(PER_CHUNK):
             expert(e)
         u = UNITS - 1
         for i in range(PER_CHUNK):
             weave(gathered(u), woven(u), i * C, (i + 1) * C)
             quantize(codes[u], scales[u], woven(u), i * C, (i + 1) * C)
+        quantize_shared(2)
         for e in range(PER_CHUNK, E):
             expert(e)
-        quantize_shared(2, shared_stage[:])
-        quantize_shared(LAST, stage[2][:])
+        quantize_shared(LAST)
         shared()
 
-        gate_a = ring.tile([P, 2, T], F32, name="x_raw", bufs=4)
+        gate_a = ring.tile([P, 2, T], F32, name="x_raw")
         nc.sync.dma_start(out=gate_a[:], in_=gate[0:2].rearrange("r n t -> n r t"))
-        gate_b = ring.tile([P, 2, T], F32, name="x_raw", bufs=4)
+        gate_b = ring.tile([P, 2, T], F32, name="x_raw")
         nc.sync.dma_start(out=gate_b[:, 0, :], in_=gate[2])
         gates = [gate_a[:, 0, :], gate_a[:, 1, :], gate_b[:, 0, :]]
 
-        for half in range(2):
-            cols = slice(half * HALF, (half + 1) * HALF)
-            pos_cols = slice(half * HALF // 16, (half + 1) * HALF // 16)
-            parts = late[half][:].bitcast(F32).rearrange("p (r t) -> p r t", t=HALF)
-            for r in range(3):
-                nc.vector.tensor_tensor(parts[:, r, :], y[:].indirect(pos_sb[r][:, pos_cols]), gates[r][:, cols], MULT)
-            nc.vector.tensor_tensor(parts[:, 3, :], parts[:, 0, :], parts[:, 1, :], ADD)
-            nc.vector.tensor_tensor(parts[:, 4, :], parts[:, 3, :], parts[:, 2, :], ADD)
-            nc.vector.tensor_tensor(parts[:, 5, :], parts[:, 4, :], ys[:, cols], ADD)
-            nc.sync.dma_start(out=out[:, cols], in_=parts[:, 5, :])
+        def cols(half):
+            return slice(half * HALF, (half + 1) * HALF)
+
+        def fetch(half, r):
+            offsets = pos_sb[r][:, half * HALF // 16 : (half + 1) * HALF // 16]
+            nc.vector.tensor_tensor(parts[half][:, r, :], y[:].indirect(offsets), gates[r][:, cols(half)], MULT)
+
+        def add(half, row, left, right):
+            nc.vector.tensor_tensor(parts[half][:, row, :], left, right, ADD)
+
+        first, second = parts
+        for r in range(3):
+            fetch(0, r)
+        add(0, 3, first[:, 0, :], first[:, 1, :])
+        fetch(1, 0)
+        add(0, 4, first[:, 3, :], first[:, 2, :])
+        fetch(1, 1)
+        add(0, 5, first[:, 4, :], ys[:, cols(0)])
+        nc.sync.dma_start(out=out[:, cols(0)], in_=first[:, 5, :])
+        add(1, 3, second[:, 0, :], ys[:, cols(1)])
+        fetch(1, 2)
+        add(1, 4, second[:, 3, :], second[:, 1, :])
+        add(1, 5, second[:, 4, :], second[:, 2, :])
+        nc.sync.dma_start(out=out[:, cols(1)], in_=second[:, 5, :])

@@ -14,6 +14,7 @@ U8 = mybir.dt.uint8
 FP8X4 = mybir.dt.float8_e4m3fn_x4
 MULT = mybir.AluOpType.mult
 ADD = mybir.AluOpType.add
+COPY = mybir.ActivationFunctionType.Copy
 SILU = mybir.ActivationFunctionType.Silu
 
 P = 128
@@ -27,13 +28,15 @@ WINDOW = 1024
 HALF = T // 2
 
 
-UNITS = PASSES * CHUNKS
+SCALAR_UNIT = (0, CHUNKS - 1)
+UNIT_LIST = [(g, c) for g in range(PASSES) for c in range(CHUNKS) if (g, c) != SCALAR_UNIT]
+UNITS = len(UNIT_LIST)
 LAST = PASSES - 1
 W_COLS = PASSES * N
 ROW_W = 4
 ROW_SHARED = 8
 ROW_W_SHARED = 12
-GPSIMD_COLS = 80
+GPSIMD_COLS = 96
 
 
 def tile_moe_shr_lin_silu_kernel(tc, xT, w, b, gate, offs, pos1, pos2, pos3, out):
@@ -59,11 +62,19 @@ def tile_moe_shr_lin_silu_kernel(tc, xT, w, b, gate, offs, pos1, pos2, pos3, out
         scales = [rows[:, C:] for rows in scale_rows]
         shared_codes = [keep.tile([P, T], U32, name="shared_codes%d" % g, align_bytes=64) for g in range(PASSES)]
         w_codes = [keep.tile([P, W_COLS], U32, name="w_codes%d" % e, align_bytes=64) for e in range(E + 1)]
-        shared_scales = [scale_rows[u][ROW_SHARED:, :T] for u in (0, CHUNKS, UNITS - 1)]
+        shared_scales = [scale_rows[u][ROW_SHARED:, :T] for u in (0, 2, UNITS - 1)]
         shared_scales.append(scale_rows[UNITS - 1][ROW_W_SHARED:, :T])
         w_order = [E] + list(range(E))
         w_scales = {e: scale_rows[i + 1][(ROW_W if e < E else ROW_W_SHARED) :, :W_COLS] for i, e in enumerate(w_order)}
-        parts = [keep.tile([P, 6, HALF], F32, name="parts%d" % i) for i in range(2)]
+        w_scales[w_order[E]] = scale_rows[E][ROW_W_SHARED:, :W_COLS]
+        parts = [keep.tile([P, 6 * HALF], F32, name="parts%d" % i, align_bytes=64) for i in range(2)]
+        singles = [keep.tile([P, T], BF16, name="single%d" % j, align_bytes=64) for j in range(PACK)]
+        picked = parts[0][:, : 2 * CHUNK].bitcast(BF16)
+        picked_woven = parts[1][:, : 2 * CHUNK].bitcast(U32)
+        picked_codes = keep.tile([P, CHUNK], U32, name="picked_codes", align_bytes=64)
+        picked_scales = keep.tile([P, CHUNK], U8, name="picked_scales", align_bytes=64)
+        quantized = {unit: (codes[u], scales[u]) for u, unit in enumerate(UNIT_LIST)}
+        quantized[SCALAR_UNIT] = (picked_codes, picked_scales)
 
         def plane_of(g, h):
             return planes[g % 2][:, 2 * WINDOW * h : 2 * WINDOW * (h + 1)]
@@ -75,19 +86,20 @@ def tile_moe_shr_lin_silu_kernel(tc, xT, w, b, gate, offs, pos1, pos2, pos3, out
         x_raw = {}
         w_raw = {}
 
-        def load_x(g, h):
+        def load_x(g, h, pieces=((0, T),)):
             x_raw[g, h] = ring.tile([P, 2, T], F32, name="x_raw")
             rows = xT[g * K_PASS : (g + 1) * K_PASS, :].rearrange("(p j) t -> p j t", j=PACK)
-            nc.sync.dma_start(out=x_raw[g, h][:], in_=rows[:, 2 * h : 2 * h + 2, :])
+            for lo, hi in pieces:
+                nc.sync.dma_start(out=x_raw[g, h][:, :, lo:hi], in_=rows[:, 2 * h : 2 * h + 2, lo:hi])
 
         def load_w(i):
             w_raw[i] = ring.tile([P, PASSES, PACK * N], F32, name="w_raw")
             nc.sync.dma_start(out=w_raw[i][:], in_=w[w_order[i]].rearrange("(g p j) n -> p g (j n)", p=P, j=PACK))
 
-        def cast_x(g, h, copy):
+        def cast_x(g, h, copy, lo=0, hi=T):
             copy(
-                out=plane_of(g, h)[:, : 2 * T].rearrange("p (t j) -> p t j", j=2),
-                in_=x_raw[g, h][:].rearrange("p j t -> p t j"),
+                out=plane_of(g, h)[:, 2 * lo : 2 * hi].rearrange("p (t j) -> p t j", j=2),
+                in_=x_raw[g, h][:, :, lo:hi].rearrange("p j t -> p t j"),
             )
 
         def cast_w_scalar(i):
@@ -114,12 +126,35 @@ def tile_moe_shr_lin_silu_kernel(tc, xT, w, b, gate, offs, pos1, pos2, pos3, out
             return stage[(u + 2) % 3][:]
 
         def gather(u):
-            g, c = divmod(u, CHUNKS)
+            g, c = UNIT_LIST[u]
             offsets = offs_sb[:, c * CHUNK // 16 : (c + 1) * CHUNK // 16]
             for h in range(2):
                 nc.vector.tensor_copy(
                     out=gathered(u)[:, h * CHUNK : (h + 1) * CHUNK], in_=plane_of(g, h).bitcast(U32).indirect(offsets)
                 )
+
+        def split_on_gpsimd(j):
+            pairs = plane_of(0, 0)[:, : 2 * T].rearrange("p (t j) -> p t j", j=2)
+            nc.gpsimd.tensor_scalar(singles[j][:], pairs[:, :, j], 1.0, 0.0, MULT, ADD)
+
+        def cast_single(j):
+            nc.scalar.copy(out=singles[j][:], in_=x_raw[0, j // 2][:, j % 2, :])
+
+        def pick(n):
+            half, j = divmod(n, PACK)
+            first = SCALAR_UNIT[1] * CHUNK + half * HALF
+            nc.scalar.activation(
+                out=picked[:, j * CHUNK + half * HALF : j * CHUNK + (half + 1) * HALF],
+                in_=singles[j][:].indirect(offs_sb[:, first // 16 : (first + HALF) // 16]),
+                func=COPY,
+            )
+
+        def weave_picked(half):
+            slots = slice(half * HALF, (half + 1) * HALF)
+            nc.scalar.copy(
+                out=picked_woven.bitcast(BF16).rearrange("p (s j) -> p s j", j=PACK)[:, slots, :],
+                in_=picked.rearrange("p (j s) -> p s j", j=PACK)[:, slots, :],
+            )
 
         def quantize(dst, plane, src, lo, hi):
             nc.vector.quantize_mx(
@@ -140,7 +175,8 @@ def tile_moe_shr_lin_silu_kernel(tc, xT, w, b, gate, offs, pos1, pos2, pos3, out
             quantize(shared_codes[g], shared_scales[g], shared_woven[g], 512, T)
 
         def product(e, operands, lo, width, acc, dst):
-            for g in range(PASSES):
+            order = [1, 2, 0, 3]
+            for g in order:
                 moving, plane = operands[g]
                 nc.tensor.matmul_mx(
                     out=acc[:],
@@ -148,7 +184,7 @@ def tile_moe_shr_lin_silu_kernel(tc, xT, w, b, gate, offs, pos1, pos2, pos3, out
                     lhsT_scale=w_scales[e][:, g * N : (g + 1) * N],
                     rhs=moving[:, lo : lo + width].bitcast(FP8X4),
                     rhs_scale=plane[:, lo : lo + width],
-                    start=(g == 0),
+                    start=(g == order[0]),
                     stop=(g == LAST),
                 )
             nc.scalar.activation(out=dst, in_=acc[:], func=SILU, bias=b_sb[:, e : e + 1])
@@ -156,7 +192,7 @@ def tile_moe_shr_lin_silu_kernel(tc, xT, w, b, gate, offs, pos1, pos2, pos3, out
         def expert(e):
             c, i = divmod(e, PER_CHUNK)
             acc = psum.tile([P, C], F32, name="acc", bufs=6)
-            operands = [(codes[g * CHUNKS + c], scales[g * CHUNKS + c]) for g in range(PASSES)]
+            operands = [quantized[g, c] for g in range(PASSES)]
             product(e, operands, i * C, C, acc, y[:, e * C : (e + 1) * C])
 
         def shared():
@@ -165,32 +201,34 @@ def tile_moe_shr_lin_silu_kernel(tc, xT, w, b, gate, offs, pos1, pos2, pos3, out
                 acc_shared = psum.tile([P, width], F32, name="acc_shared", bufs=2)
                 product(E, operands, lo, width, acc_shared, ys[:, lo : lo + width])
 
-        load_x(0, 0)
+        load_x(0, 0, ((0, HALF), (HALF, T)))
         nc.sync.dma_start(offs_sb[:], offs)
         load_x(0, 1)
         load_w(0)
         load_x(1, 0)
-        load_w(1)
         load_x(1, 1)
+        load_w(1)
         nc.sync.dma_start(b_sb[:], b)
         for r, pos in enumerate((pos1, pos2, pos3)):
             nc.sync.dma_start(pos_sb[r][:], pos)
         load_w(2)
         load_w(3)
 
-        cast_x(0, 0, nc.vector.tensor_copy)
+        cast_x(0, 0, nc.vector.tensor_copy, 0, HALF)
+        cast_x(0, 0, nc.vector.tensor_copy, HALF, T)
         cast_x(0, 1, nc.scalar.copy)
         load_x(2, 0)
-        load_x(2, 1)
         gather(0)
         gather(1)
+        split_on_gpsimd(0)
+        split_on_gpsimd(1)
         cast_w_gpsimd(0)
+        cast_single(2)
         weave_shared(0)
 
         for u in range(UNITS - 1):
-            g, c = divmod(u, CHUNKS)
             weave(gathered(u), woven(u), 0, CHUNK)
-            if u == CHUNKS:
+            if u == 2:
                 quantize_shared(1)
             quantize(codes[u], scales[u], woven(u), 0, C)
             quantize(codes[u], scales[u], woven(u), C, 2 * C)
@@ -200,21 +238,35 @@ def tile_moe_shr_lin_silu_kernel(tc, xT, w, b, gate, offs, pos1, pos2, pos3, out
             quantize(codes[u], scales[u], woven(u), 2 * C, CHUNK)
             if u == 0:
                 quantize_shared(0)
+            if u == 0:
+                cast_x(1, 0, nc.scalar.copy)
+                load_x(2, 1)
+            g, step = divmod(u + 1, CHUNKS)
             if g < LAST:
-                if c < 2:
-                    cast_x(g + 1, c, nc.scalar.copy)
-                    if g + 3 < PASSES:
-                        load_x(g + 3, c)
+                if step < 2:
+                    cast_x(g + 1, step, nc.scalar.copy)
+                    if u == 0:
+                        load_x(LAST, 1)
+                    if u == 2:
+                        cast_single(3)
+                        load_x(LAST, 0)
                 else:
                     weave_shared(g + 1)
-            if u <= E:
-                cast_w_scalar(u)
-                if u + 4 <= E:
-                    load_w(u + 4)
+            cast_w_scalar(u)
+            if u + 4 <= E:
+                load_w(u + 4)
+            if 1 <= u <= 2 * PACK:
+                pick(u - 1)
+            if u >= 8:
+                weave_picked(u - 8)
             if u + 2 < UNITS:
                 gather(u + 2)
             if u + 1 <= E:
                 cast_w_gpsimd(u + 1)
+        e = w_order[E]
+        nc.vector.quantize_mx(out=w_codes[e][:].bitcast(FP8X4), scales=w_scales[e], in_=w_cast[E % 2])
+        quantize(picked_codes, picked_scales, picked_woven, 0, 512)
+        quantize(picked_codes, picked_scales, picked_woven, 512, CHUNK)
         for e in range(PER_CHUNK):
             expert(e)
         u = UNITS - 1
@@ -232,6 +284,8 @@ def tile_moe_shr_lin_silu_kernel(tc, xT, w, b, gate, offs, pos1, pos2, pos3, out
         gate_b = ring.tile([P, 2, T], F32, name="x_raw")
         nc.sync.dma_start(out=gate_b[:, 0, :], in_=gate[2])
         gates = [gate_a[:, 0, :], gate_a[:, 1, :], gate_b[:, 0, :]]
+
+        parts = [part[:].rearrange("p (r t) -> p r t", t=HALF) for part in parts]
 
         def cols(half):
             return slice(half * HALF, (half + 1) * HALF)

@@ -1,8 +1,10 @@
 from contextlib import ExitStack
 
 import concourse.mybir as mybir
+from concourse.masks import make_identity
 
 K, T, E, C, N = 2048, 768, 9, 256, 128
+TOP = 3
 SLOTS = E * C
 FLOPS = 2 * K * N * (SLOTS + T)
 
@@ -19,61 +21,78 @@ SILU = mybir.ActivationFunctionType.Silu
 
 P = 128
 PACK = 4
+LIST_ROWS = 16
 K_PASS = P * PACK
 PASSES = K // K_PASS
+LAST_PASS = PASSES - 1
 CHUNK = 768
 CHUNKS = SLOTS // CHUNK
 PER_CHUNK = CHUNK // C
 WINDOW = 1024
 HALF = T // 2
-
+BANK = 512
+W_COLS = PASSES * N
 
 SCALAR_UNIT = (0, CHUNKS - 1)
-UNIT_LIST = [(g, c) for g in range(PASSES) for c in range(CHUNKS) if (g, c) != SCALAR_UNIT]
-UNITS = len(UNIT_LIST)
-LAST = PASSES - 1
-W_COLS = PASSES * N
-ROW_W = 4
-ROW_SHARED = 8
-ROW_W_SHARED = 12
+VECTOR_UNITS = [(g, c) for g in range(PASSES) for c in range(CHUNKS) if (g, c) != SCALAR_UNIT]
+STEPS = len(VECTOR_UNITS)
+SCALAR_GATHERS = 2 * PACK
+PASS_ORDER = list(range(1, LAST_PASS)) + [0, LAST_PASS]
+W_ORDER = [E] + list(range(E))
+
+ROW_4, ROW_8, ROW_12 = 4, 8, 12
+
 GPSIMD_COLS = 96
+FRONT = 512
+BACK = T - FRONT
+
+AHEAD = 2
+STAGES = AHEAD + 1
+RING = 4
+EXPERT_BANKS, SHARED_BANKS = 6, 2
 
 
 def tile_moe_shr_lin_silu_kernel(tc, xT, w, b, gate, offs, pos1, pos2, pos3, out):
     nc = tc.nc
     with ExitStack() as ctx:
         keep = ctx.enter_context(tc.tile_pool(name="keep", bufs=1))
-        ring = ctx.enter_context(tc.tile_pool(name="ring", bufs=4))
+        ring = ctx.enter_context(tc.tile_pool(name="ring", bufs=RING))
         psum = ctx.enter_context(tc.psum_pool(name="psum", bufs=1))
 
-        offs_sb = keep.tile([P, SLOTS // 16], U16, name="offs_sb")
-        pos_sb = [keep.tile([P, T // 16], U16, name="pos_sb%d" % r) for r in range(3)]
+        def kept(name, count, width, dtype):
+            return [keep.tile([P, width], dtype, name="%s%d" % (name, i), align_bytes=64) for i in range(count)]
+
+        offs_sb = keep.tile([P, SLOTS // LIST_ROWS], U16, name="offs_sb")
+        pos_sb = [keep.tile([P, T // LIST_ROWS], U16, name="pos_sb%d" % r) for r in range(TOP)]
         b_sb = keep.tile([P, E + 1], F32, name="b_sb")
         y = keep.tile([P, SLOTS], F32, name="y")
         ys = keep.tile([P, T], F32, name="ys")
-        planes = [keep.tile([P, 4 * WINDOW], BF16, name="planes%d" % i, align_bytes=64) for i in range(2)]
-        stage = [keep.tile([P, 2 * CHUNK], U32, name="stage%d" % i, align_bytes=64) for i in range(3)]
-        w_bf = [keep.tile([P, PACK * T], BF16, name="w_bf%d" % i, align_bytes=64) for i in range(2)]
-        shared_stage = [keep.tile([P, 2 * T], U32, name="shared_stage%d" % i, align_bytes=64) for i in range(2)]
-        shared_woven = [w_bf[1][:].bitcast(U32), shared_stage[1][:], shared_stage[0][:], shared_stage[1][:]]
-        w_cast = [buf[:, PACK * (T - W_COLS) :] for buf in w_bf]
-        codes = [keep.tile([P, CHUNK], U32, name="codes%d" % u, align_bytes=64) for u in range(UNITS)]
-        scale_rows = [keep.tile([P, C + CHUNK], U8, name="scale_rows%d" % u, align_bytes=64) for u in range(UNITS)]
-        scales = [rows[:, C:] for rows in scale_rows]
-        shared_codes = [keep.tile([P, T], U32, name="shared_codes%d" % g, align_bytes=64) for g in range(PASSES)]
-        w_codes = [keep.tile([P, W_COLS], U32, name="w_codes%d" % e, align_bytes=64) for e in range(E + 1)]
-        shared_scales = [scale_rows[u][ROW_SHARED:, :T] for u in (0, 2, UNITS - 1)]
-        shared_scales.append(scale_rows[UNITS - 1][ROW_W_SHARED:, :T])
-        w_order = [E] + list(range(E))
-        w_scales = {e: scale_rows[i + 1][(ROW_W if e < E else ROW_W_SHARED) :, :W_COLS] for i, e in enumerate(w_order)}
-        w_scales[w_order[E]] = scale_rows[E][ROW_W_SHARED:, :W_COLS]
-        parts = [keep.tile([P, 6 * HALF], F32, name="parts%d" % i, align_bytes=64) for i in range(2)]
-        singles = [keep.tile([P, T], BF16, name="single%d" % j, align_bytes=64) for j in range(PACK)]
-        picked = parts[0][:, : 2 * CHUNK].bitcast(BF16)
-        picked_woven = parts[1][:, : 2 * CHUNK].bitcast(U32)
+        planes = kept("planes", 2, PACK * WINDOW, BF16)
+        stage = kept("stage", STAGES, 2 * CHUNK, U32)
+        w_tiles = kept("w_bf", 2, PACK * T, BF16)
+        shared_stage = kept("shared_stage", 2, 2 * T, U32)
+        codes = kept("codes", STEPS, CHUNK, U32)
+        scale_rows = kept("scale_rows", STEPS, C + CHUNK, U8)
+        shared_codes = kept("shared_codes", PASSES, T, U32)
+        w_codes = kept("w_codes", E + 1, W_COLS, U32)
+        work = kept("parts", 2, 6 * HALF, F32)
+        singles = kept("single", PACK, T, BF16)
         picked_codes = keep.tile([P, CHUNK], U32, name="picked_codes", align_bytes=64)
         picked_scales = keep.tile([P, CHUNK], U8, name="picked_scales", align_bytes=64)
-        quantized = {unit: (codes[u], scales[u]) for u, unit in enumerate(UNIT_LIST)}
+
+        w_cast = [tile[:, PACK * (T - W_COLS) :] for tile in w_tiles]
+        shared_woven = [w_tiles[1][:].bitcast(U32), shared_stage[1][:], shared_stage[0][:], shared_stage[1][:]]
+        picked = work[0][:, : 2 * CHUNK].bitcast(BF16)
+        picked_woven = work[1][:, : 2 * CHUNK].bitcast(U32)
+
+        scales = [rows[:, C:] for rows in scale_rows]
+        shared_1_step = CHUNKS - 1
+        shared_scales = [scale_rows[s][ROW_8:, :T] for s in (0, shared_1_step, STEPS - 1)]
+        shared_scales.append(scale_rows[STEPS - 1][ROW_12:, :T])
+        w_scales = {e: scale_rows[i + 1][ROW_4:, :W_COLS] for i, e in enumerate(W_ORDER)}
+        w_scales[E] = scale_rows[1][ROW_12:, :W_COLS]
+        w_scales[W_ORDER[E]] = scale_rows[E][ROW_12:, :W_COLS]
+        quantized = {unit: (codes[s], scales[s]) for s, unit in enumerate(VECTOR_UNITS)}
         quantized[SCALAR_UNIT] = (picked_codes, picked_scales)
 
         def plane_of(g, h):
@@ -82,6 +101,9 @@ def tile_moe_shr_lin_silu_kernel(tc, xT, w, b, gate, offs, pos1, pos2, pos3, out
         for g in range(2):
             for h in range(2):
                 nc.gpsimd.memset(plane_of(g, h)[:, 2 * T :].bitcast(U32), 0)
+
+        identity = keep.tile([P, P], F32, name="identity")
+        make_identity(nc, identity[:])
 
         x_raw = {}
         w_raw = {}
@@ -94,7 +116,7 @@ def tile_moe_shr_lin_silu_kernel(tc, xT, w, b, gate, offs, pos1, pos2, pos3, out
 
         def load_w(i):
             w_raw[i] = ring.tile([P, PASSES, PACK * N], F32, name="w_raw")
-            nc.sync.dma_start(out=w_raw[i][:], in_=w[w_order[i]].rearrange("(g p j) n -> p g (j n)", p=P, j=PACK))
+            nc.sync.dma_start(out=w_raw[i][:], in_=w[W_ORDER[i]].rearrange("(g p j) n -> p g (j n)", p=P, j=PACK))
 
         def cast_x(g, h, copy, lo=0, hi=T):
             copy(
@@ -109,43 +131,41 @@ def tile_moe_shr_lin_silu_kernel(tc, xT, w, b, gate, offs, pos1, pos2, pos3, out
                 in_=w_raw[i][:].rearrange("p g (j c i) -> p g c j i", j=PACK, i=4)[:, :, first:],
             )
 
+        def copy_on_gpsimd(dst, src):
+            nc.gpsimd.tensor_scalar(dst, src, 1.0, 0.0, MULT, ADD)
+
         def cast_w_gpsimd(i):
-            nc.gpsimd.tensor_scalar(
+            copy_on_gpsimd(
                 w_cast[i % 2].rearrange("p (g n j) -> p g n j", n=N, j=PACK)[:, :, :GPSIMD_COLS],
                 w_raw[i][:].rearrange("p g (j n) -> p g n j", j=PACK)[:, :, :GPSIMD_COLS],
-                1.0,
-                0.0,
-                MULT,
-                ADD,
             )
 
-        def gathered(u):
-            return stage[u % 3][:]
+        def gathered(s):
+            return stage[s % STAGES][:]
 
-        def woven(u):
-            return stage[(u + 2) % 3][:]
+        def woven(s):
+            return gathered(s + AHEAD)
 
-        def gather(u):
-            g, c = UNIT_LIST[u]
-            offsets = offs_sb[:, c * CHUNK // 16 : (c + 1) * CHUNK // 16]
+        def entries(list_tile, lo, hi):
+            return list_tile[:, lo // LIST_ROWS : hi // LIST_ROWS]
+
+        def gather(s):
+            g, c = VECTOR_UNITS[s]
+            offsets = entries(offs_sb, c * CHUNK, (c + 1) * CHUNK)
             for h in range(2):
                 nc.vector.tensor_copy(
-                    out=gathered(u)[:, h * CHUNK : (h + 1) * CHUNK], in_=plane_of(g, h).bitcast(U32).indirect(offsets)
+                    out=gathered(s)[:, h * CHUNK : (h + 1) * CHUNK], in_=plane_of(g, h).bitcast(U32).indirect(offsets)
                 )
-
-        def split_on_gpsimd(j):
-            pairs = plane_of(0, 0)[:, : 2 * T].rearrange("p (t j) -> p t j", j=2)
-            nc.gpsimd.tensor_scalar(singles[j][:], pairs[:, :, j], 1.0, 0.0, MULT, ADD)
 
         def cast_single(j):
             nc.scalar.copy(out=singles[j][:], in_=x_raw[0, j // 2][:, j % 2, :])
 
-        def pick(n):
+        def gather_on_scalar(n):
             half, j = divmod(n, PACK)
             first = SCALAR_UNIT[1] * CHUNK + half * HALF
             nc.scalar.activation(
                 out=picked[:, j * CHUNK + half * HALF : j * CHUNK + (half + 1) * HALF],
-                in_=singles[j][:].indirect(offs_sb[:, first // 16 : (first + HALF) // 16]),
+                in_=singles[j][:].indirect(entries(offs_sb, first, first + HALF)),
                 func=COPY,
             )
 
@@ -154,11 +174,6 @@ def tile_moe_shr_lin_silu_kernel(tc, xT, w, b, gate, offs, pos1, pos2, pos3, out
             nc.scalar.copy(
                 out=picked_woven.bitcast(BF16).rearrange("p (s j) -> p s j", j=PACK)[:, slots, :],
                 in_=picked.rearrange("p (j s) -> p s j", j=PACK)[:, slots, :],
-            )
-
-        def quantize(dst, plane, src, lo, hi):
-            nc.vector.quantize_mx(
-                out=dst[:, lo:hi].bitcast(FP8X4), scales=plane[:, lo:hi], in_=src.bitcast(BF16)[:, PACK * lo : PACK * hi]
             )
 
         def weave(src, dst, lo, hi):
@@ -170,13 +185,27 @@ def tile_moe_shr_lin_silu_kernel(tc, xT, w, b, gate, offs, pos1, pos2, pos3, out
         def weave_shared(g):
             weave(planes[g % 2][:].bitcast(U32), shared_woven[g], 0, T)
 
+        def quantize(dst, plane, src, lo, hi):
+            nc.vector.quantize_mx(
+                out=dst[:, lo:hi].bitcast(FP8X4), scales=plane[:, lo:hi], in_=src.bitcast(BF16)[:, PACK * lo : PACK * hi]
+            )
+
+        def quantize_whole(dst, plane, src):
+            quantize(dst, plane, src, 0, BANK)
+            quantize(dst, plane, src, BANK, CHUNK)
+
         def quantize_shared(g):
-            quantize(shared_codes[g], shared_scales[g], shared_woven[g], 0, 512)
-            quantize(shared_codes[g], shared_scales[g], shared_woven[g], 512, T)
+            quantize_whole(shared_codes[g], shared_scales[g], shared_woven[g])
+
+        def quantize_expert(s, i):
+            quantize(codes[s], scales[s], woven(s), i * C, (i + 1) * C)
+
+        def quantize_w(i):
+            e = W_ORDER[i]
+            nc.vector.quantize_mx(out=w_codes[e][:].bitcast(FP8X4), scales=w_scales[e], in_=w_cast[i % 2])
 
         def product(e, operands, lo, width, acc, dst):
-            order = [1, 2, 0, 3]
-            for g in order:
+            for g in PASS_ORDER:
                 moving, plane = operands[g]
                 nc.tensor.matmul_mx(
                     out=acc[:],
@@ -184,22 +213,22 @@ def tile_moe_shr_lin_silu_kernel(tc, xT, w, b, gate, offs, pos1, pos2, pos3, out
                     lhsT_scale=w_scales[e][:, g * N : (g + 1) * N],
                     rhs=moving[:, lo : lo + width].bitcast(FP8X4),
                     rhs_scale=plane[:, lo : lo + width],
-                    start=(g == order[0]),
-                    stop=(g == LAST),
+                    start=(g == PASS_ORDER[0]),
+                    stop=(g == PASS_ORDER[-1]),
                 )
             nc.scalar.activation(out=dst, in_=acc[:], func=SILU, bias=b_sb[:, e : e + 1])
 
         def expert(e):
             c, i = divmod(e, PER_CHUNK)
-            acc = psum.tile([P, C], F32, name="acc", bufs=6)
+            acc = psum.tile([P, C], F32, name="acc", bufs=EXPERT_BANKS)
             operands = [quantized[g, c] for g in range(PASSES)]
             product(e, operands, i * C, C, acc, y[:, e * C : (e + 1) * C])
 
-        def shared():
-            operands = [(shared_codes[g], shared_scales[g]) for g in range(PASSES)]
-            for lo, width in ((0, 512), (512, 256)):
-                acc_shared = psum.tile([P, width], F32, name="acc_shared", bufs=2)
-                product(E, operands, lo, width, acc_shared, ys[:, lo : lo + width])
+        def shared_expert():
+            operands = list(zip(shared_codes, shared_scales))
+            for lo, hi in ((0, BANK), (BANK, T)):
+                acc_shared = psum.tile([P, hi - lo], F32, name="acc_shared", bufs=SHARED_BANKS)
+                product(E, operands, lo, hi - lo, acc_shared, ys[:, lo:hi])
 
         load_x(0, 0, ((0, HALF), (HALF, T)))
         nc.sync.dma_start(offs_sb[:], offs)
@@ -218,66 +247,67 @@ def tile_moe_shr_lin_silu_kernel(tc, xT, w, b, gate, offs, pos1, pos2, pos3, out
         cast_x(0, 0, nc.vector.tensor_copy, HALF, T)
         cast_x(0, 1, nc.scalar.copy)
         load_x(2, 0)
-        gather(0)
-        gather(1)
-        split_on_gpsimd(0)
-        split_on_gpsimd(1)
+        for s in range(AHEAD):
+            gather(s)
+        first_pairs = plane_of(0, 0)[:, : 2 * T].rearrange("p (t j) -> p t j", j=2)
+        for j in range(2):
+            copy_on_gpsimd(singles[j][:], first_pairs[:, :, j])
         cast_w_gpsimd(0)
         cast_single(2)
         weave_shared(0)
 
-        for u in range(UNITS - 1):
-            weave(gathered(u), woven(u), 0, CHUNK)
-            if u == 2:
+        for s in range(STEPS - 1):
+            weave(gathered(s), woven(s), 0, CHUNK)
+            if s == shared_1_step:
                 quantize_shared(1)
-            quantize(codes[u], scales[u], woven(u), 0, C)
-            quantize(codes[u], scales[u], woven(u), C, 2 * C)
-            if u >= 1:
-                e = w_order[u - 1]
-                nc.vector.quantize_mx(out=w_codes[e][:].bitcast(FP8X4), scales=w_scales[e], in_=w_cast[(u - 1) % 2])
-            quantize(codes[u], scales[u], woven(u), 2 * C, CHUNK)
-            if u == 0:
+            quantize_expert(s, 0)
+            quantize_expert(s, 1)
+            if s >= 1:
+                quantize_w(s - 1)
+            quantize_expert(s, 2)
+            if s == 0:
                 quantize_shared(0)
-            if u == 0:
                 cast_x(1, 0, nc.scalar.copy)
                 load_x(2, 1)
-            g, step = divmod(u + 1, CHUNKS)
-            if g < LAST:
-                if step < 2:
-                    cast_x(g + 1, step, nc.scalar.copy)
-                    if u == 0:
-                        load_x(LAST, 1)
-                    if u == 2:
+
+            g, job = divmod(s + 1, CHUNKS)
+            if g < LAST_PASS:
+                if job < 2:
+                    cast_x(g + 1, job, nc.scalar.copy)
+                    if s == 0:
+                        load_x(LAST_PASS, 1)
+                    if s == shared_1_step:
                         cast_single(3)
-                        load_x(LAST, 0)
+                        load_x(LAST_PASS, 0)
                 else:
                     weave_shared(g + 1)
-            cast_w_scalar(u)
-            if u + 4 <= E:
-                load_w(u + 4)
-            if 1 <= u <= 2 * PACK:
-                pick(u - 1)
-            if u >= 8:
-                weave_picked(u - 8)
-            if u + 2 < UNITS:
-                gather(u + 2)
-            if u + 1 <= E:
-                cast_w_gpsimd(u + 1)
-        e = w_order[E]
-        nc.vector.quantize_mx(out=w_codes[e][:].bitcast(FP8X4), scales=w_scales[e], in_=w_cast[E % 2])
-        quantize(picked_codes, picked_scales, picked_woven, 0, 512)
-        quantize(picked_codes, picked_scales, picked_woven, 512, CHUNK)
+            cast_w_scalar(s)
+            if s + RING <= E:
+                load_w(s + RING)
+            if 1 <= s <= SCALAR_GATHERS:
+                gather_on_scalar(s - 1)
+            if s >= SCALAR_GATHERS:
+                weave_picked(s - SCALAR_GATHERS)
+
+            if s + AHEAD < STEPS:
+                gather(s + AHEAD)
+            if s + 1 <= E:
+                cast_w_gpsimd(s + 1)
+
+        quantize_w(E)
+        quantize_whole(picked_codes, picked_scales, picked_woven)
         for e in range(PER_CHUNK):
             expert(e)
-        u = UNITS - 1
+
+        s = STEPS - 1
         for i in range(PER_CHUNK):
-            weave(gathered(u), woven(u), i * C, (i + 1) * C)
-            quantize(codes[u], scales[u], woven(u), i * C, (i + 1) * C)
-        quantize_shared(2)
+            weave(gathered(s), woven(s), i * C, (i + 1) * C)
+            quantize_expert(s, i)
+        quantize_shared(LAST_PASS - 1)
         for e in range(PER_CHUNK, E):
             expert(e)
-        quantize_shared(LAST)
-        shared()
+        quantize_shared(LAST_PASS)
+        shared_expert()
 
         gate_a = ring.tile([P, 2, T], F32, name="x_raw")
         nc.sync.dma_start(out=gate_a[:], in_=gate[0:2].rearrange("r n t -> n r t"))
@@ -285,29 +315,39 @@ def tile_moe_shr_lin_silu_kernel(tc, xT, w, b, gate, offs, pos1, pos2, pos3, out
         nc.sync.dma_start(out=gate_b[:, 0, :], in_=gate[2])
         gates = [gate_a[:, 0, :], gate_a[:, 1, :], gate_b[:, 0, :]]
 
-        parts = [part[:].rearrange("p (r t) -> p r t", t=HALF) for part in parts]
+        def fetch(dst, r, lo, hi):
+            nc.vector.tensor_tensor(dst, y[:].indirect(entries(pos_sb[r], lo, hi)), gates[r][:, lo:hi], MULT)
 
-        def cols(half):
-            return slice(half * HALF, (half + 1) * HALF)
+        terms = work[0][:, : TOP * FRONT].rearrange("p (r t) -> p r t", r=TOP)
+        front_out = work[0][:, TOP * FRONT : (TOP + 1) * FRONT]
+        turned = stage[0][:].bitcast(F32)
+        blocks = [slice(t, t + P) for t in range(0, FRONT, P)]
+        for r in range(TOP):
+            fetch(terms[:, r, :], r, 0, FRONT)
+        sums = [psum.tile([P, P], F32, name="acc", bufs=EXPERT_BANKS) for block in blocks]
+        addends = [terms[:, 0, :], terms[:, 1, :], ys[:, :FRONT], terms[:, 2, :]]
+        for a, addend in enumerate(addends):
+            for total, block in zip(sums, blocks):
+                nc.tensor.matmul(
+                    total[:],
+                    addend[:, block],
+                    identity[:],
+                    start=(a == 0),
+                    stop=(a == len(addends) - 1),
+                    is_transpose=True,
+                )
+        upright = psum.tile([P, FRONT], F32, name="acc_shared", bufs=SHARED_BANKS)
+        for total, block in zip(sums, blocks):
+            nc.scalar.copy(out=turned[:, block], in_=total[:])
+            nc.tensor.transpose(upright[:, block], turned[:, block], identity[:])
+        nc.scalar.copy(out=front_out, in_=upright[:])
+        nc.sync.dma_start(out=out[:, :FRONT], in_=front_out)
 
-        def fetch(half, r):
-            offsets = pos_sb[r][:, half * HALF // 16 : (half + 1) * HALF // 16]
-            nc.vector.tensor_tensor(parts[half][:, r, :], y[:].indirect(offsets), gates[r][:, cols(half)], MULT)
-
-        def add(half, row, left, right):
-            nc.vector.tensor_tensor(parts[half][:, row, :], left, right, ADD)
-
-        first, second = parts
-        for r in range(3):
-            fetch(0, r)
-        add(0, 3, first[:, 0, :], first[:, 1, :])
-        fetch(1, 0)
-        add(0, 4, first[:, 3, :], first[:, 2, :])
-        fetch(1, 1)
-        add(0, 5, first[:, 4, :], ys[:, cols(0)])
-        nc.sync.dma_start(out=out[:, cols(0)], in_=first[:, 5, :])
-        add(1, 3, second[:, 0, :], ys[:, cols(1)])
-        fetch(1, 2)
-        add(1, 4, second[:, 3, :], second[:, 1, :])
-        add(1, 5, second[:, 4, :], second[:, 2, :])
-        nc.sync.dma_start(out=out[:, cols(1)], in_=second[:, 5, :])
+        term_1, term_2, term_3, sum_1, sum_2, back_out = [work[1][:, i * BACK : (i + 1) * BACK] for i in range(6)]
+        fetch(term_1, 0, FRONT, T)
+        fetch(term_2, 1, FRONT, T)
+        nc.vector.tensor_tensor(sum_1, term_1, ys[:, FRONT:], ADD)
+        fetch(term_3, 2, FRONT, T)
+        nc.vector.tensor_tensor(sum_2, sum_1, term_2, ADD)
+        nc.vector.tensor_tensor(back_out, sum_2, term_3, ADD)
+        nc.sync.dma_start(out=out[:, FRONT:], in_=back_out)

from contextlib import ExitStack

import concourse.mybir as mybir
from concourse.masks import make_identity

K, T, E, C, N = 2048, 768, 9, 256, 128
TOP = 3
SLOTS = E * C
FLOPS = 2 * K * N * (SLOTS + T)

F32 = mybir.dt.float32
BF16 = mybir.dt.bfloat16
U32 = mybir.dt.uint32
U16 = mybir.dt.uint16
U8 = mybir.dt.uint8
FP8X4 = mybir.dt.float8_e4m3fn_x4
MULT = mybir.AluOpType.mult
ADD = mybir.AluOpType.add
COPY = mybir.ActivationFunctionType.Copy
SILU = mybir.ActivationFunctionType.Silu

P = 128
PACK = 4
LIST_ROWS = 16
K_PASS = P * PACK
PASSES = K // K_PASS
LAST_PASS = PASSES - 1
CHUNK = 768
CHUNKS = SLOTS // CHUNK
PER_CHUNK = CHUNK // C
WINDOW = 1024
HALF = T // 2
BANK = 512
W_COLS = PASSES * N

SCALAR_UNIT = (0, CHUNKS - 1)
VECTOR_UNITS = [(g, c) for g in range(PASSES) for c in range(CHUNKS) if (g, c) != SCALAR_UNIT]
STEPS = len(VECTOR_UNITS)
SCALAR_GATHERS = 2 * PACK
PASS_ORDER = list(range(1, LAST_PASS)) + [0, LAST_PASS]
W_ORDER = [E] + list(range(E))

ROW_4, ROW_8, ROW_12 = 4, 8, 12

GPSIMD_COLS = 96
FRONT = 512
BACK = T - FRONT

AHEAD = 2
STAGES = AHEAD + 1
RING = 4
EXPERT_BANKS, SHARED_BANKS = 6, 2


def tile_moe_shr_lin_silu_kernel(tc, xT, w, b, gate, offs, pos1, pos2, pos3, out):
    nc = tc.nc
    with ExitStack() as ctx:
        keep = ctx.enter_context(tc.tile_pool(name="keep", bufs=1))
        ring = ctx.enter_context(tc.tile_pool(name="ring", bufs=RING))
        psum = ctx.enter_context(tc.psum_pool(name="psum", bufs=1))

        def kept(name, count, width, dtype):
            return [keep.tile([P, width], dtype, name="%s%d" % (name, i), align_bytes=64) for i in range(count)]

        offs_sb = keep.tile([P, SLOTS // LIST_ROWS], U16, name="offs_sb")
        pos_sb = [keep.tile([P, T // LIST_ROWS], U16, name="pos_sb%d" % r) for r in range(TOP)]
        b_sb = keep.tile([P, E + 1], F32, name="b_sb")
        y = keep.tile([P, SLOTS], F32, name="y")
        ys = keep.tile([P, T], F32, name="ys")
        planes = kept("planes", 2, PACK * WINDOW, BF16)
        stage = kept("stage", STAGES, 2 * CHUNK, U32)
        w_tiles = kept("w_bf", 2, PACK * T, BF16)
        shared_stage = kept("shared_stage", 2, 2 * T, U32)
        codes = kept("codes", STEPS, CHUNK, U32)
        scale_rows = kept("scale_rows", STEPS, C + CHUNK, U8)
        shared_codes = kept("shared_codes", PASSES, T, U32)
        w_codes = kept("w_codes", E + 1, W_COLS, U32)
        work = kept("parts", 2, 6 * HALF, F32)
        singles = kept("single", PACK, T, BF16)
        picked_codes = keep.tile([P, CHUNK], U32, name="picked_codes", align_bytes=64)
        picked_scales = keep.tile([P, CHUNK], U8, name="picked_scales", align_bytes=64)

        w_cast = [tile[:, PACK * (T - W_COLS) :] for tile in w_tiles]
        shared_woven = [w_tiles[1][:].bitcast(U32), shared_stage[1][:], shared_stage[0][:], shared_stage[1][:]]
        picked = work[0][:, : 2 * CHUNK].bitcast(BF16)
        picked_woven = work[1][:, : 2 * CHUNK].bitcast(U32)

        scales = [rows[:, C:] for rows in scale_rows]
        shared_1_step = CHUNKS - 1
        shared_scales = [scale_rows[s][ROW_8:, :T] for s in (0, shared_1_step, STEPS - 1)]
        shared_scales.append(scale_rows[STEPS - 1][ROW_12:, :T])
        w_scales = {e: scale_rows[i + 1][ROW_4:, :W_COLS] for i, e in enumerate(W_ORDER)}
        w_scales[E] = scale_rows[1][ROW_12:, :W_COLS]
        w_scales[W_ORDER[E]] = scale_rows[E][ROW_12:, :W_COLS]
        quantized = {unit: (codes[s], scales[s]) for s, unit in enumerate(VECTOR_UNITS)}
        quantized[SCALAR_UNIT] = (picked_codes, picked_scales)

        def plane_of(g, h):
            return planes[g % 2][:, 2 * WINDOW * h : 2 * WINDOW * (h + 1)]

        for g in range(2):
            for h in range(2):
                nc.gpsimd.memset(plane_of(g, h)[:, 2 * T :].bitcast(U32), 0)

        identity = keep.tile([P, P], F32, name="identity")
        make_identity(nc, identity[:])

        x_raw = {}
        w_raw = {}

        def load_x(g, h, pieces=((0, T),)):
            x_raw[g, h] = ring.tile([P, 2, T], F32, name="x_raw")
            rows = xT[g * K_PASS : (g + 1) * K_PASS, :].rearrange("(p j) t -> p j t", j=PACK)
            for lo, hi in pieces:
                nc.sync.dma_start(out=x_raw[g, h][:, :, lo:hi], in_=rows[:, 2 * h : 2 * h + 2, lo:hi])

        def load_w(i):
            w_raw[i] = ring.tile([P, PASSES, PACK * N], F32, name="w_raw")
            nc.sync.dma_start(out=w_raw[i][:], in_=w[W_ORDER[i]].rearrange("(g p j) n -> p g (j n)", p=P, j=PACK))

        def cast_x(g, h, copy, lo=0, hi=T):
            copy(
                out=plane_of(g, h)[:, 2 * lo : 2 * hi].rearrange("p (t j) -> p t j", j=2),
                in_=x_raw[g, h][:, :, lo:hi].rearrange("p j t -> p t j"),
            )

        def cast_w_scalar(i):
            first = GPSIMD_COLS // 4
            nc.scalar.copy(
                out=w_cast[i % 2].rearrange("p (g c i j) -> p g c j i", g=PASSES, i=4, j=PACK)[:, :, first:],
                in_=w_raw[i][:].rearrange("p g (j c i) -> p g c j i", j=PACK, i=4)[:, :, first:],
            )

        def copy_on_gpsimd(dst, src):
            nc.gpsimd.tensor_scalar(dst, src, 1.0, 0.0, MULT, ADD)

        def cast_w_gpsimd(i):
            copy_on_gpsimd(
                w_cast[i % 2].rearrange("p (g n j) -> p g n j", n=N, j=PACK)[:, :, :GPSIMD_COLS],
                w_raw[i][:].rearrange("p g (j n) -> p g n j", j=PACK)[:, :, :GPSIMD_COLS],
            )

        def gathered(s):
            return stage[s % STAGES][:]

        def woven(s):
            return gathered(s + AHEAD)

        def entries(list_tile, lo, hi):
            return list_tile[:, lo // LIST_ROWS : hi // LIST_ROWS]

        def gather(s):
            g, c = VECTOR_UNITS[s]
            offsets = entries(offs_sb, c * CHUNK, (c + 1) * CHUNK)
            for h in range(2):
                nc.vector.tensor_copy(
                    out=gathered(s)[:, h * CHUNK : (h + 1) * CHUNK], in_=plane_of(g, h).bitcast(U32).indirect(offsets)
                )

        def cast_single(j):
            nc.scalar.copy(out=singles[j][:], in_=x_raw[0, j // 2][:, j % 2, :])

        def gather_on_scalar(n):
            half, j = divmod(n, PACK)
            first = SCALAR_UNIT[1] * CHUNK + half * HALF
            nc.scalar.activation(
                out=picked[:, j * CHUNK + half * HALF : j * CHUNK + (half + 1) * HALF],
                in_=singles[j][:].indirect(entries(offs_sb, first, first + HALF)),
                func=COPY,
            )

        def weave_picked(half):
            slots = slice(half * HALF, (half + 1) * HALF)
            nc.scalar.copy(
                out=picked_woven.bitcast(BF16).rearrange("p (s j) -> p s j", j=PACK)[:, slots, :],
                in_=picked.rearrange("p (j s) -> p s j", j=PACK)[:, slots, :],
            )

        def weave(src, dst, lo, hi):
            nc.scalar.copy(
                out=dst.rearrange("p (s h) -> p s h", h=2)[:, lo:hi, :],
                in_=src.rearrange("p (h s) -> p s h", h=2)[:, lo:hi, :],
            )

        def weave_shared(g):
            weave(planes[g % 2][:].bitcast(U32), shared_woven[g], 0, T)

        def quantize(dst, plane, src, lo, hi):
            nc.vector.quantize_mx(
                out=dst[:, lo:hi].bitcast(FP8X4), scales=plane[:, lo:hi], in_=src.bitcast(BF16)[:, PACK * lo : PACK * hi]
            )

        def quantize_whole(dst, plane, src):
            quantize(dst, plane, src, 0, BANK)
            quantize(dst, plane, src, BANK, CHUNK)

        def quantize_shared(g):
            quantize_whole(shared_codes[g], shared_scales[g], shared_woven[g])

        def quantize_expert(s, i):
            quantize(codes[s], scales[s], woven(s), i * C, (i + 1) * C)

        def quantize_w(i):
            e = W_ORDER[i]
            nc.vector.quantize_mx(out=w_codes[e][:].bitcast(FP8X4), scales=w_scales[e], in_=w_cast[i % 2])

        def product(e, operands, lo, width, acc, dst):
            for g in PASS_ORDER:
                moving, plane = operands[g]
                nc.tensor.matmul_mx(
                    out=acc[:],
                    lhsT=w_codes[e][:, g * N : (g + 1) * N].bitcast(FP8X4),
                    lhsT_scale=w_scales[e][:, g * N : (g + 1) * N],
                    rhs=moving[:, lo : lo + width].bitcast(FP8X4),
                    rhs_scale=plane[:, lo : lo + width],
                    start=(g == PASS_ORDER[0]),
                    stop=(g == PASS_ORDER[-1]),
                )
            nc.scalar.activation(out=dst, in_=acc[:], func=SILU, bias=b_sb[:, e : e + 1])

        def expert(e):
            c, i = divmod(e, PER_CHUNK)
            acc = psum.tile([P, C], F32, name="acc", bufs=EXPERT_BANKS)
            operands = [quantized[g, c] for g in range(PASSES)]
            product(e, operands, i * C, C, acc, y[:, e * C : (e + 1) * C])

        def shared_expert():
            operands = list(zip(shared_codes, shared_scales))
            for lo, hi in ((0, BANK), (BANK, T)):
                acc_shared = psum.tile([P, hi - lo], F32, name="acc_shared", bufs=SHARED_BANKS)
                product(E, operands, lo, hi - lo, acc_shared, ys[:, lo:hi])

        load_x(0, 0, ((0, HALF), (HALF, T)))
        nc.sync.dma_start(offs_sb[:], offs)
        load_x(0, 1)
        load_w(0)
        load_x(1, 0)
        load_x(1, 1)
        load_w(1)
        nc.sync.dma_start(b_sb[:], b)
        for r, pos in enumerate((pos1, pos2, pos3)):
            nc.sync.dma_start(pos_sb[r][:], pos)
        load_w(2)
        load_w(3)

        cast_x(0, 0, nc.vector.tensor_copy, 0, HALF)
        cast_x(0, 0, nc.vector.tensor_copy, HALF, T)
        cast_x(0, 1, nc.scalar.copy)
        load_x(2, 0)
        for s in range(AHEAD):
            gather(s)
        first_pairs = plane_of(0, 0)[:, : 2 * T].rearrange("p (t j) -> p t j", j=2)
        for j in range(2):
            copy_on_gpsimd(singles[j][:], first_pairs[:, :, j])
        cast_w_gpsimd(0)
        cast_single(2)
        weave_shared(0)

        for s in range(STEPS - 1):
            weave(gathered(s), woven(s), 0, CHUNK)
            if s == shared_1_step:
                quantize_shared(1)
            quantize_expert(s, 0)
            quantize_expert(s, 1)
            if s >= 1:
                quantize_w(s - 1)
            quantize_expert(s, 2)
            if s == 0:
                quantize_shared(0)
                cast_x(1, 0, nc.scalar.copy)
                load_x(2, 1)

            g, job = divmod(s + 1, CHUNKS)
            if g < LAST_PASS:
                if job < 2:
                    cast_x(g + 1, job, nc.scalar.copy)
                    if s == 0:
                        load_x(LAST_PASS, 1)
                    if s == shared_1_step:
                        cast_single(3)
                        load_x(LAST_PASS, 0)
                else:
                    weave_shared(g + 1)
            cast_w_scalar(s)
            if s + RING <= E:
                load_w(s + RING)
            if 1 <= s <= SCALAR_GATHERS:
                gather_on_scalar(s - 1)
            if s >= SCALAR_GATHERS:
                weave_picked(s - SCALAR_GATHERS)

            if s + AHEAD < STEPS:
                gather(s + AHEAD)
            if s + 1 <= E:
                cast_w_gpsimd(s + 1)

        quantize_w(E)
        quantize_whole(picked_codes, picked_scales, picked_woven)
        for e in range(PER_CHUNK):
            expert(e)

        s = STEPS - 1
        for i in range(PER_CHUNK):
            weave(gathered(s), woven(s), i * C, (i + 1) * C)
            quantize_expert(s, i)
        quantize_shared(LAST_PASS - 1)
        for e in range(PER_CHUNK, E):
            expert(e)
        quantize_shared(LAST_PASS)
        shared_expert()

        gate_a = ring.tile([P, 2, T], F32, name="x_raw")
        nc.sync.dma_start(out=gate_a[:], in_=gate[0:2].rearrange("r n t -> n r t"))
        gate_b = ring.tile([P, 2, T], F32, name="x_raw")
        nc.sync.dma_start(out=gate_b[:, 0, :], in_=gate[2])
        gates = [gate_a[:, 0, :], gate_a[:, 1, :], gate_b[:, 0, :]]

        def fetch(dst, r, lo, hi):
            nc.vector.tensor_tensor(dst, y[:].indirect(entries(pos_sb[r], lo, hi)), gates[r][:, lo:hi], MULT)

        terms = work[0][:, : TOP * FRONT].rearrange("p (r t) -> p r t", r=TOP)
        front_out = work[0][:, TOP * FRONT : (TOP + 1) * FRONT]
        turned = stage[0][:].bitcast(F32)
        blocks = [slice(t, t + P) for t in range(0, FRONT, P)]
        for r in range(TOP):
            fetch(terms[:, r, :], r, 0, FRONT)
        sums = [psum.tile([P, P], F32, name="acc", bufs=EXPERT_BANKS) for block in blocks]
        addends = [terms[:, 0, :], terms[:, 1, :], ys[:, :FRONT], terms[:, 2, :]]
        for a, addend in enumerate(addends):
            for total, block in zip(sums, blocks):
                nc.tensor.matmul(
                    total[:],
                    addend[:, block],
                    identity[:],
                    start=(a == 0),
                    stop=(a == len(addends) - 1),
                    is_transpose=True,
                )
        upright = psum.tile([P, FRONT], F32, name="acc_shared", bufs=SHARED_BANKS)
        for total, block in zip(sums, blocks):
            nc.scalar.copy(out=turned[:, block], in_=total[:])
            nc.tensor.transpose(upright[:, block], turned[:, block], identity[:])
        nc.scalar.copy(out=front_out, in_=upright[:])
        nc.sync.dma_start(out=out[:, :FRONT], in_=front_out)

        term_1, term_2, term_3, sum_1, sum_2, back_out = [work[1][:, i * BACK : (i + 1) * BACK] for i in range(6)]
        fetch(term_1, 0, FRONT, T)
        fetch(term_2, 1, FRONT, T)
        nc.vector.tensor_tensor(sum_1, term_1, ys[:, FRONT:], ADD)
        fetch(term_3, 2, FRONT, T)
        nc.vector.tensor_tensor(sum_2, sum_1, term_2, ADD)
        nc.vector.tensor_tensor(back_out, sum_2, term_3, ADD)
        nc.sync.dma_start(out=out[:, FRONT:], in_=back_out)
